import numpy as np
import ml_dtypes


def mxq(x, axis, fmt="e4m3"):
    dtype, down = {"e4m3": (ml_dtypes.float8_e4m3fn, 7), "e5m2": (ml_dtypes.float8_e5m2, 14)}[fmt]
    v = np.moveaxis(np.asarray(x, np.float32).astype(ml_dtypes.bfloat16).astype(np.float64), axis, -1)
    blocks = v.reshape(v.shape[:-1] + (-1, 32))
    amax = np.abs(blocks).max(-1, keepdims=True)
    byte = np.maximum(np.where(amax > 0, np.frexp(amax)[1] - 1 + 127, 0) - down, 1)
    scale = np.exp2(byte - 127.0)
    codes = (blocks / scale).astype(np.float32).astype(dtype).astype(np.float64)
    return np.moveaxis((codes * scale).reshape(v.shape), -1, axis)


WIDE = False


def mx_kscale(k):
    if not WIDE:
        return np.ones(k)
    levels = np.array([10, -10, 5, -5, 0])
    if k % 512:
        return np.exp2(np.random.permutation(np.resize(levels, k // 32))).repeat(32)
    a = np.empty((k // 512, 16))
    for p in range(k // 512):
        a[p, :8] = np.random.permutation(np.resize(levels, 8))
        for g in range(8):
            far = levels[np.abs(levels - a[p, g]) >= 10]
            a[p, g + 8] = far[np.random.randint(len(far))]
    return np.exp2(a.ravel()).repeat(32)


def f64(x):
    return np.asarray(x).astype(np.float64)


def striped(idx):
    return np.tile(idx.reshape(-1, 16).T, (8, 1)).astype(np.uint16)


def unstriped(offs):
    return offs[:16].T.reshape(-1).astype(np.int64)


E2M1 = np.array([0.0, 0.5, 1.0, 1.5, 2.0, 3.0, 4.0, 6.0, -0.0, -0.5, -1.0, -1.5, -2.0, -3.0, -4.0, -6.0])


def pack_weight(w, fmt):
    k, n = w.shape
    w = f64(np.asarray(w, np.float32).astype(ml_dtypes.bfloat16)).reshape(k // 32, 32, n)
    amax = np.abs(w).max(1)
    if fmt == "e4m3":
        byte = np.frexp(amax)[1] - 1 + 127 - 7
    else:
        mant, ex = np.frexp(amax / 6.0)
        byte = np.where(mant > 0.5, ex, ex - 1) + 127
    byte = np.clip(np.where(amax > 0, byte, 1), 1, 254)
    scaled = (w * np.exp2(127.0 - byte)[:, None, :]).reshape(k, n).astype(np.float32)
    by_word = np.ascontiguousarray(scaled.reshape(k // 512, 128, 4, n).transpose(0, 1, 3, 2))
    if fmt == "e4m3":
        words = by_word.astype(ml_dtypes.float8_e4m3fn).view(np.uint8)
    else:
        c = by_word.astype(ml_dtypes.float4_e2m1fn).view(np.uint8) & 0xF
        words = (c[..., 0::2] | (c[..., 1::2] << 4)).reshape(k // 512, 128, 2 * n)
    return np.ascontiguousarray(words), np.ascontiguousarray(byte.astype(np.uint8).reshape(k // 512, 16, n))


def unpack_weight(words, scales, fmt):
    g, _, n = scales.shape
    words = np.ascontiguousarray(words).reshape(g, 128, n, -1)
    if fmt == "e4m3":
        vals = words.view(ml_dtypes.float8_e4m3fn).astype(np.float64)
    else:
        nib = np.empty((g, 128, n, 4), np.uint8)
        nib[..., 0::2] = words & 0xF
        nib[..., 1::2] = words >> 4
        vals = E2M1[nib]
    vals = vals * np.repeat(np.exp2(scales.astype(np.float64) - 127.0), 8, axis=1)[..., None]
    return vals.transpose(0, 1, 3, 2).reshape(g * 512, n)


def pack_table(v):
    words, scales = pack_weight(v, "e4m3")
    return np.concatenate([words.reshape(words.shape[0], -1), scales.reshape(scales.shape[0], -1)], axis=1)


def unpack_table(tab):
    g, t = tab.shape[0], tab.shape[1] // 528
    return unpack_weight(tab[:, :512 * t].reshape(g, 128, t, 4), tab[:, 512 * t:].reshape(g, 16, t), "e4m3")


def gelu(v):
    return 0.5 * v * (1.0 + np.tanh(np.sqrt(2.0 / np.pi) * (v + 0.044715 * v**3)))


K, M, T, S = 2048, 512, 2048, 512


def setup_inputs():
    n = np.random.standard_normal
    s = mx_kscale(K)[:, None]
    p_w4 = pack_weight(n((K, M)) / np.sqrt(K) / s, "e2m1")
    return {
        "tab": pack_table(n((K, T)) * s),
        "w4_words": p_w4[0],
        "w4_scales": p_w4[1],
        "dw": (0.3 * n((K, M)) / np.sqrt(K) / s).astype(np.float32),
        "b": (0.3 * n(512)).astype(np.float32),
        "offs": striped(np.random.permutation(T)[:S]),
    }


def reference(tab, w4_words, w4_scales, dw, b, offs):
    tab_ = unpack_table(tab)[:, unstriped(offs)]
    w4_ = unpack_weight(w4_words, w4_scales, "e2m1")
    dw_ = mxq(f64(dw), 0, "e4m3")
    y = w4_.T @ tab_ + dw_.T @ tab_
    return gelu(y + f64(b)[:, None])

@@ -1,0 +1,177 @@
+from contextlib import ExitStack
+
+import concourse.mybir as mybir
+
+K, M, T, S = 2048, 512, 2048, 512
+FLOPS = 2 * 2 * K * M * S
+
+F32 = mybir.dt.float32
+BF16 = mybir.dt.bfloat16
+I32 = mybir.dt.int32
+U32 = mybir.dt.uint32
+U16 = mybir.dt.uint16
+U8 = mybir.dt.uint8
+FP8X4 = mybir.dt.float8_e4m3fn_x4
+FP4X4 = mybir.dt.float4_e2m1fn_x4
+GELU = mybir.ActivationFunctionType.Gelu_apprx_tanh
+
+P = 128
+PASSES = K // 512
+MT = M // P
+TAIL = ((2, 0, 256, 128), (3, 0, 256, 128), (2, 256, 512, 384), (3, 256, 384, 256), (3, 384, 512, 384))
+
+
+def tile_list_tabd_gelu_kernel(tc, tab, w4_words, w4_scales, dw, b, offs, out):
+    nc = tc.nc
+    with ExitStack() as ctx:
+        keep = ctx.enter_context(tc.tile_pool(name="keep", bufs=1))
+        psum = ctx.enter_context(tc.psum_pool(name="psum", bufs=1))
+
+        offsets = keep.tile([P, S // 16], U16, name="offsets")
+
+        w4s = keep.tile([P, PASSES, M], U8, name="w4s", align_bytes=64)
+        tabs = keep.tile([P, T], U8, name="tabs", align_bytes=64)
+        gp = keep.tile([P, S], U8, name="gp", align_bytes=64)
+        gs = keep.tile([P, PASSES - 1, S], U8, name="gs", align_bytes=64)
+        nc.vector.memset(tabs[:].bitcast(I32), 0)
+        nc.vector.memset(w4s[:].bitcast(I32), 0)
+        nc.vector.memset(gs[:].bitcast(I32), 0)
+
+        warm = keep.tile([P, 1], F32, name="warm")
+        nc.vector.memset(warm[:], 0.0)
+        brow = keep.tile([P, 32], F32, name="brow", align_bytes=64)
+        bias = keep.tile([P, 32], F32, name="bias", align_bytes=64)
+        nc.vector.memset(brow[:], 0.0)
+        warm_out = keep.tile([P, 1], F32, name="warm_out")
+        nc.scalar.activation(warm_out[:], warm[:], GELU)
+
+        raw = [keep.tile([P, 4, M], F32, name=f"raw{a}") for a in range(PASSES)]
+        words = [keep.tile([P, T], I32, name=f"words{a}") for a in range(PASSES)]
+        w4 = keep.tile([P, PASSES, 2 * M], U8, name="w4", align_bytes=64)
+
+        def load_dw(a, c0, c1):
+            nc.sync.dma_start(
+                raw[a][:, :, c0:c1],
+                dw[512 * a : 512 * (a + 1), c0:c1].rearrange("(p j) n -> p j n", j=4),
+            )
+
+        def load_words(a):
+            nc.sync.dma_start(words[a][:], tab[a, 0 : 512 * T].rearrange("(p n) -> p n", p=P).bitcast(I32))
+
+        for q in range(4):
+            nc.scalar.dma_start(
+                tabs[32 * q : 32 * q + 16, :].bitcast(I32),
+                tab[:, (512 + 4 * q) * T : (516 + 4 * q) * T].rearrange("a (r t) -> a r t", t=T).bitcast(I32),
+            )
+        for q in range(4):
+            nc.gpsimd.dma_start(
+                w4s[32 * q : 32 * q + 4, :, :].bitcast(I32),
+                w4_scales[:, 4 * q : 4 * q + 4, :].rearrange("a r n -> r a n").bitcast(I32),
+            )
+        for q in range(4):
+            nc.gpsimd.dma_start(brow[32 * q : 32 * q + MT, :], b.rearrange("(m q i) -> q m i", q=4, i=32)[q, :, :])
+        load_dw(0, 0, M)
+        nc.sync.dma_start(offsets[:], offs)
+        load_words(0)
+        nc.sync.dma_start(w4[:].bitcast(I32), w4_words.rearrange("a p n -> p a n").bitcast(I32))
+        load_dw(1, 0, M)
+        load_words(1)
+        load_words(2)
+
+        def shift(engine, a):
+            for q in range(4):
+                engine.dma_start(
+                    gs[32 * q : 32 * q + 4, a - 1, :].bitcast(I32),
+                    gp[32 * q + 4 * a : 32 * q + 4 * a + 4, :].bitcast(I32),
+                )
+
+        nc.vector.tensor_copy(gp[:], tabs[:].indirect(offsets[:]))
+        shift(nc.scalar, 1)
+        shift(nc.gpsimd, 2)
+        shift(nc.gpsimd, 3)
+        load_words(3)
+        load_dw(2, 0, 256)
+        load_dw(3, 0, 256)
+        load_dw(2, 256, 512)
+        load_dw(3, 256, 384)
+        load_dw(3, 384, 512)
+
+        acc = [psum.tile([P, S], F32, name=f"acc{m}") for m in range(MT)]
+        dq = [keep.tile([P, M], U32, name=f"dq{a}", align_bytes=64) for a in range(PASSES)]
+        ds = [keep.tile([P, M], U8, name=f"ds{a}", align_bytes=64) for a in range(PASSES)]
+        bf = [keep.tile([P, M, 4], BF16, name=f"bf{a}", align_bytes=64) for a in range(PASSES)]
+        gw = [keep.tile([P, S], U32, name=f"gw{a}", align_bytes=64) for a in range(PASSES)]
+
+        def interleave(engine_copy, a, c0, c1):
+            engine_copy(bf[a][:, c0:c1, :], raw[a][:, :, c0:c1].rearrange("p j n -> p n j"))
+
+        def quantize(a, c0, c1):
+            nc.vector.quantize_mx(
+                out=dq[a][:, c0:c1].bitcast(FP8X4),
+                scales=ds[a][:, c0:c1],
+                in_=bf[a][:, c0:c1, :].rearrange("p n j -> p (n j)"),
+            )
+
+        def base_passes(a):
+            for m in range(MT):
+                nc.tensor.matmul_mx(
+                    out=acc[m][:],
+                    lhsT=w4[:, a, 256 * m : 256 * (m + 1)].bitcast(FP4X4),
+                    lhsT_scale=w4s[:, a, P * m : P * (m + 1)],
+                    rhs=gw[a][:].bitcast(FP8X4),
+                    rhs_scale=gp[:] if a == 0 else gs[:, a - 1, :],
+                    start=(a == 0),
+                    stop=False,
+                )
+
+        def change_passes(a, ms):
+            for m in ms:
+                nc.tensor.matmul_mx(
+                    out=acc[m][:],
+                    lhsT=dq[a][:, P * m : P * (m + 1)].bitcast(FP8X4),
+                    lhsT_scale=ds[a][:, P * m : P * (m + 1)],
+                    rhs=gw[a][:].bitcast(FP8X4),
+                    rhs_scale=gp[4 * a : P, :],
+                    start=False,
+                    stop=(a == PASSES - 1),
+                )
+
+        def finish(m):
+            res = keep.tile([P, S], F32, name=f"res{m}")
+            nc.scalar.activation(res[:], acc[m][:], GELU, bias=bias[:, m : m + 1])
+            nc.sync.dma_start(out[P * m : P * (m + 1), :], res[:])
+
+        def gather_words(a):
+            nc.vector.tensor_copy(gw[a][:], words[a][:].bitcast(U32).indirect(offsets[:]))
+
+        interleave(nc.scalar.copy, 0, 0, M)
+        gather_words(0)
+        base_passes(0)
+        quantize(0, 0, M)
+        change_passes(0, range(MT))
+
+        interleave(nc.scalar.copy, 1, 0, M)
+        nc.vector.transpose(bias[:], brow[:])
+
+        gather_words(1)
+        quantize(1, 0, M)
+        change_passes(1, range(MT))
+        base_passes(1)
+        gather_words(2)
+        base_passes(2)
+        gather_words(3)
+        base_passes(3)
+
+        for a, c0, c1, cut in TAIL:
+            if cut > c0:
+                interleave(nc.scalar.copy, a, c0, cut)
+            interleave(nc.vector.tensor_copy, a, cut, c1)
+            quantize(a, c0, c1)
+            if (a, c0) == (2, 256):
+                finish(0)
+                finish(1)
+            ms = range(c0 // P, c1 // P)
+            change_passes(a, ms)
+            if a == PASSES - 1 and c0 >= 256:
+                for m in ms:
+                    finish(m)

@@ -18,7 +18,7 @@ GELU = mybir.ActivationFunctionType.Gelu_apprx_tanh
 P = 128
 PASSES = K // 512
 MT = M // P
-TAIL = ((2, 0, 256, 128), (3, 0, 256, 128), (2, 256, 512, 384), (3, 256, 384, 256), (3, 384, 512, 384))
+LAST = PASSES - 1
 
 
 def tile_list_tabd_gelu_kernel(tc, tab, w4_words, w4_scales, dw, b, offs, out):
@@ -28,150 +28,119 @@ def tile_list_tabd_gelu_kernel(tc, tab, w4_words, w4_scales, dw, b, offs, out):
         psum = ctx.enter_context(tc.psum_pool(name="psum", bufs=1))
 
         offsets = keep.tile([P, S // 16], U16, name="offsets")
-
-        w4s = keep.tile([P, PASSES, M], U8, name="w4s", align_bytes=64)
         tabs = keep.tile([P, T], U8, name="tabs", align_bytes=64)
-        gp = keep.tile([P, S], U8, name="gp", align_bytes=64)
-        gs = keep.tile([P, PASSES - 1, S], U8, name="gs", align_bytes=64)
-        nc.vector.memset(tabs[:].bitcast(I32), 0)
-        nc.vector.memset(w4s[:].bitcast(I32), 0)
-        nc.vector.memset(gs[:].bitcast(I32), 0)
+        picked = keep.tile([P, S], U8, name="picked", align_bytes=64)
+        stage = keep.tile([P, S + M], U8, name="stage", align_bytes=64)
+        planes = keep.tile([P, PASSES, S + M], U8, name="planes", align_bytes=64)
+        brow = keep.tile([P, 32], F32, name="brow", align_bytes=64)
+        nc.vector.memset(brow[:], 0.0)
+        nc.vector.memset(tabs[64:P, :].bitcast(I32), 0)
+        nc.vector.memset(planes[:].bitcast(I32), 0)
 
         warm = keep.tile([P, 1], F32, name="warm")
         nc.vector.memset(warm[:], 0.0)
-        brow = keep.tile([P, 32], F32, name="brow", align_bytes=64)
-        bias = keep.tile([P, 32], F32, name="bias", align_bytes=64)
-        nc.vector.memset(brow[:], 0.0)
         warm_out = keep.tile([P, 1], F32, name="warm_out")
         nc.scalar.activation(warm_out[:], warm[:], GELU)
 
-        raw = [keep.tile([P, 4, M], F32, name=f"raw{a}") for a in range(PASSES)]
+        raw = [keep.tile([P, 4, M], F32, name=f"raw{a}", align_bytes=64) for a in range(LAST)]
+        raw_last = [keep.tile([P, 4, P], F32, name=f"raw_last{m}") for m in range(MT)]
         words = [keep.tile([P, T], I32, name=f"words{a}") for a in range(PASSES)]
         w4 = keep.tile([P, PASSES, 2 * M], U8, name="w4", align_bytes=64)
 
-        def load_dw(a, c0, c1):
-            nc.sync.dma_start(
-                raw[a][:, :, c0:c1],
-                dw[512 * a : 512 * (a + 1), c0:c1].rearrange("(p j) n -> p j n", j=4),
-            )
+        def load_dw(dst, a, c0, c1):
+            nc.sync.dma_start(dst[:], dw[512 * a : 512 * (a + 1), c0:c1].rearrange("(p j) n -> p j n", j=4))
 
         def load_words(a):
             nc.sync.dma_start(words[a][:], tab[a, 0 : 512 * T].rearrange("(p n) -> p n", p=P).bitcast(I32))
 
-        for q in range(4):
-            nc.scalar.dma_start(
-                tabs[32 * q : 32 * q + 16, :].bitcast(I32),
-                tab[:, (512 + 4 * q) * T : (516 + 4 * q) * T].rearrange("a (r t) -> a r t", t=T).bitcast(I32),
-            )
-        for q in range(4):
-            nc.gpsimd.dma_start(
-                w4s[32 * q : 32 * q + 4, :, :].bitcast(I32),
-                w4_scales[:, 4 * q : 4 * q + 4, :].rearrange("a r n -> r a n").bitcast(I32),
-            )
-        for q in range(4):
-            nc.gpsimd.dma_start(brow[32 * q : 32 * q + MT, :], b.rearrange("(m q i) -> q m i", q=4, i=32)[q, :, :])
-        load_dw(0, 0, M)
+        nc.sync.dma_start(
+            tabs[0:64, :].bitcast(I32),
+            tab[:, 512 * T : 528 * T].rearrange("a (r t) -> r a t", t=T).bitcast(I32),
+        )
         nc.sync.dma_start(offsets[:], offs)
+        nc.sync.dma_start(stage[0:64, S : S + M].bitcast(I32), w4_scales.rearrange("a r n -> r a n").bitcast(I32))
+        nc.gpsimd.dma_start(brow[0:P:8, :], b.rearrange("(m q i) -> q m i", q=4, i=32))
+        load_dw(raw[0], 0, 0, M)
         load_words(0)
         nc.sync.dma_start(w4[:].bitcast(I32), w4_words.rearrange("a p n -> p a n").bitcast(I32))
-        load_dw(1, 0, M)
-        load_words(1)
-        load_words(2)
+        for a in range(1, LAST):
+            load_dw(raw[a], a, 0, M)
+            load_words(a)
+        load_words(LAST)
+        for m in range(MT):
+            load_dw(raw_last[m], LAST, P * m, P * (m + 1))
 
-        def shift(engine, a):
-            for q in range(4):
-                engine.dma_start(
-                    gs[32 * q : 32 * q + 4, a - 1, :].bitcast(I32),
-                    gp[32 * q + 4 * a : 32 * q + 4 * a + 4, :].bitcast(I32),
-                )
-
-        nc.vector.tensor_copy(gp[:], tabs[:].indirect(offsets[:]))
-        shift(nc.scalar, 1)
-        shift(nc.gpsimd, 2)
-        shift(nc.gpsimd, 3)
-        load_words(3)
-        load_dw(2, 0, 256)
-        load_dw(3, 0, 256)
-        load_dw(2, 256, 512)
-        load_dw(3, 256, 384)
-        load_dw(3, 384, 512)
-
-        acc = [psum.tile([P, S], F32, name=f"acc{m}") for m in range(MT)]
-        dq = [keep.tile([P, M], U32, name=f"dq{a}", align_bytes=64) for a in range(PASSES)]
-        ds = [keep.tile([P, M], U8, name=f"ds{a}", align_bytes=64) for a in range(PASSES)]
-        bf = [keep.tile([P, M, 4], BF16, name=f"bf{a}", align_bytes=64) for a in range(PASSES)]
-        gw = [keep.tile([P, S], U32, name=f"gw{a}", align_bytes=64) for a in range(PASSES)]
-
-        def interleave(engine_copy, a, c0, c1):
-            engine_copy(bf[a][:, c0:c1, :], raw[a][:, :, c0:c1].rearrange("p j n -> p n j"))
-
-        def quantize(a, c0, c1):
-            nc.vector.quantize_mx(
-                out=dq[a][:, c0:c1].bitcast(FP8X4),
-                scales=ds[a][:, c0:c1],
-                in_=bf[a][:, c0:c1, :].rearrange("p n j -> p (n j)"),
+        nc.vector.tensor_copy(picked[:], tabs[:].indirect(offsets[:]))
+        nc.vector.tensor_copy(stage[0:64, 0:S].bitcast(I32), picked[0:64, :].bitcast(I32))
+        for q in range(4):
+            nc.gpsimd.dma_start(
+                planes[32 * q : 32 * q + 4, :, :].bitcast(I32), stage[16 * q : 16 * q + 16, :].bitcast(I32)
             )
 
-        def base_passes(a):
-            for m in range(MT):
-                nc.tensor.matmul_mx(
-                    out=acc[m][:],
-                    lhsT=w4[:, a, 256 * m : 256 * (m + 1)].bitcast(FP4X4),
-                    lhsT_scale=w4s[:, a, P * m : P * (m + 1)],
-                    rhs=gw[a][:].bitcast(FP8X4),
-                    rhs_scale=gp[:] if a == 0 else gs[:, a - 1, :],
-                    start=(a == 0),
-                    stop=False,
-                )
+        acc = [psum.tile([P, S], F32, name=f"acc{m}") for m in range(MT)]
+        gw = [keep.tile([P, S], U32, name=f"gw{a}", align_bytes=64) for a in range(PASSES)]
 
-        def change_passes(a, ms):
-            for m in ms:
-                nc.tensor.matmul_mx(
-                    out=acc[m][:],
-                    lhsT=dq[a][:, P * m : P * (m + 1)].bitcast(FP8X4),
-                    lhsT_scale=ds[a][:, P * m : P * (m + 1)],
-                    rhs=gw[a][:].bitcast(FP8X4),
-                    rhs_scale=gp[4 * a : P, :],
-                    start=False,
-                    stop=(a == PASSES - 1),
-                )
+        def interleave(engine_copy, src, width, name):
+            dst = keep.tile([P, width, 4], BF16, name=name, align_bytes=64)
+            engine_copy(
+                dst[:].rearrange("p (c i) j -> p c j i", i=4),
+                src.rearrange("p j (c i) -> p c j i", i=4),
+            )
+            return dst
+
+        def quantize(src, width, name):
+            codes = keep.tile([P, width], U32, name=name + "q", align_bytes=64)
+            scales = keep.tile([P, width], U8, name=name + "s", align_bytes=64)
+            nc.vector.quantize_mx(
+                out=codes[:].bitcast(FP8X4), scales=scales[:], in_=src[:].rearrange("p n j -> p (n j)")
+            )
+            return codes, scales
+
+        def base_pass(a, m):
+            nc.tensor.matmul_mx(
+                out=acc[m][:],
+                lhsT=w4[:, a, 256 * m : 256 * (m + 1)].bitcast(FP4X4),
+                lhsT_scale=planes[:, a, S + P * m : S + P * (m + 1)],
+                rhs=gw[a][:].bitcast(FP8X4),
+                rhs_scale=planes[:, a, 0:S],
+                start=(a == 0),
+                stop=False,
+            )
+
+        def change_pass(a, m, codes, scales):
+            nc.tensor.matmul_mx(
+                out=acc[m][:],
+                lhsT=codes.bitcast(FP8X4),
+                lhsT_scale=scales,
+                rhs=gw[a][:].bitcast(FP8X4),
+                rhs_scale=planes[:, a, 0:S],
+                start=False,
+                stop=(a == LAST),
+            )
 
         def finish(m):
             res = keep.tile([P, S], F32, name=f"res{m}")
-            nc.scalar.activation(res[:], acc[m][:], GELU, bias=bias[:, m : m + 1])
+            nc.scalar.activation(res[:], acc[m][:], GELU, bias=bias[:, 8 * m : 8 * m + 1])
             nc.sync.dma_start(out[P * m : P * (m + 1), :], res[:])
 
         def gather_words(a):
             nc.vector.tensor_copy(gw[a][:], words[a][:].bitcast(U32).indirect(offsets[:]))
 
-        interleave(nc.scalar.copy, 0, 0, M)
-        gather_words(0)
-        base_passes(0)
-        quantize(0, 0, M)
-        change_passes(0, range(MT))
+        for a in range(LAST):
+            woven = interleave(nc.scalar.copy, raw[a][:], M, f"bf{a}")
+            gather_words(a)
+            codes, scales = quantize(woven, M, f"dq{a}")
+            for m in range(MT):
+                base_pass(a, m)
+            for m in range(MT):
+                change_pass(a, m, codes[:, P * m : P * (m + 1)], scales[:, P * m : P * (m + 1)])
 
-        interleave(nc.scalar.copy, 1, 0, M)
-        nc.vector.transpose(bias[:], brow[:])
-
-        gather_words(1)
-        quantize(1, 0, M)
-        change_passes(1, range(MT))
-        base_passes(1)
-        gather_words(2)
-        base_passes(2)
-        gather_words(3)
-        base_passes(3)
-
-        for a, c0, c1, cut in TAIL:
-            if cut > c0:
-                interleave(nc.scalar.copy, a, c0, cut)
-            interleave(nc.vector.tensor_copy, a, cut, c1)
-            quantize(a, c0, c1)
-            if (a, c0) == (2, 256):
-                finish(0)
-                finish(1)
-            ms = range(c0 // P, c1 // P)
-            change_passes(a, ms)
-            if a == PASSES - 1 and c0 >= 256:
-                for m in ms:
-                    finish(m)
+        bias = raw[1][:, 0, 0:32]
+        nc.vector.transpose(bias, brow[:])
+        gather_words(LAST)
+        for m in range(MT):
+            woven = interleave(nc.vector.tensor_copy, raw_last[m][:], P, f"bf_last{m}")
+            codes, scales = quantize(woven, P, f"dq_last{m}")
+            base_pass(LAST, m)
+            change_pass(LAST, m, codes[:], scales[:])
+            finish(m)

@@ -19,17 +19,19 @@ P = 128
 PASSES = K // 512
 MT = M // P
 LAST = PASSES - 1
+CHUNK = 8192
 
 
 def tile_list_tabd_gelu_kernel(tc, tab, w4_words, w4_scales, dw, b, offs, out):
     nc = tc.nc
     with ExitStack() as ctx:
         keep = ctx.enter_context(tc.tile_pool(name="keep", bufs=1))
+        late = ctx.enter_context(tc.tile_pool(name="late", bufs=1))
         psum = ctx.enter_context(tc.psum_pool(name="psum", bufs=1))
 
         offsets = keep.tile([P, S // 16], U16, name="offsets")
         tabs = keep.tile([P, T], U8, name="tabs", align_bytes=64)
-        picked = keep.tile([P, S], U8, name="picked", align_bytes=64)
+        picked = late.tile([P, 6 * CHUNK], U8, name="picked", align_bytes=64, offset=0)
         stage = keep.tile([P, S + M], U8, name="stage", align_bytes=64)
         planes = keep.tile([P, PASSES, S + M], U8, name="planes", align_bytes=64)
         brow = keep.tile([P, 32], F32, name="brow", align_bytes=64)
@@ -42,9 +44,8 @@ def tile_list_tabd_gelu_kernel(tc, tab, w4_words, w4_scales, dw, b, offs, out):
         warm_out = keep.tile([P, 1], F32, name="warm_out")
         nc.scalar.activation(warm_out[:], warm[:], GELU)
 
-        raw = [keep.tile([P, 4, M], F32, name=f"raw{a}", align_bytes=64) for a in range(LAST)]
-        raw_last = [keep.tile([P, 4, P], F32, name=f"raw_last{m}") for m in range(MT)]
-        words = [keep.tile([P, T], I32, name=f"words{a}") for a in range(PASSES)]
+        raw = [keep.tile([P, 4, M], F32, name="raw0", align_bytes=64)]
+        words = [keep.tile([P, T], I32, name="words0", align_bytes=64)]
         w4 = keep.tile([P, PASSES, 2 * M], U8, name="w4", align_bytes=64)
 
         def load_dw(dst, a, c0, c1):
@@ -63,19 +64,32 @@ def tile_list_tabd_gelu_kernel(tc, tab, w4_words, w4_scales, dw, b, offs, out):
         load_dw(raw[0], 0, 0, M)
         load_words(0)
         nc.sync.dma_start(w4[:].bitcast(I32), w4_words.rearrange("a p n -> p a n").bitcast(I32))
-        for a in range(1, LAST):
-            load_dw(raw[a], a, 0, M)
-            load_words(a)
-        load_words(LAST)
-        for m in range(MT):
-            load_dw(raw_last[m], LAST, P * m, P * (m + 1))
 
-        nc.vector.tensor_copy(picked[:], tabs[:].indirect(offsets[:]))
-        nc.vector.tensor_copy(stage[0:64, 0:S].bitcast(I32), picked[0:64, :].bitcast(I32))
+        nc.vector.tensor_copy(picked[:, 0:S], tabs[:].indirect(offsets[:]))
+        nc.vector.tensor_copy(stage[0:64, 0:S].bitcast(I32), picked[0:64, 0:S].bitcast(I32))
         for q in range(4):
-            nc.gpsimd.dma_start(
+            nc.sync.dma_start(
                 planes[32 * q : 32 * q + 4, :, :].bitcast(I32), stage[16 * q : 16 * q + 16, :].bitcast(I32)
             )
+
+        raw.append(late.tile([P, 4, M], F32, name="raw1", align_bytes=64, offset=0))
+        for a in range(1, PASSES):
+            words.append(late.tile([P, T], I32, name=f"words{a}", align_bytes=64, offset=a * CHUNK))
+
+        def load_piece(a, c0, c1):
+            piece = late.tile(
+                [P, 4, c1 - c0], F32, name=f"piece{a}_{c0}", align_bytes=64, offset=(a + 2) * CHUNK + 16 * c0
+            )
+            load_dw(piece, a, c0, c1)
+            return piece
+
+        load_dw(raw[1], 1, 0, M)
+        load_words(1)
+        load_words(2)
+        left = {2: load_piece(2, 0, 256)}
+        load_words(LAST)
+        left[LAST] = load_piece(LAST, 0, 256)
+        right = {(a, m): load_piece(a, P * m, P * (m + 1)) for m in (2, 3) for a in (2, LAST)}
 
         acc = [psum.tile([P, S], F32, name=f"acc{m}") for m in range(MT)]
         gw = [keep.tile([P, S], U32, name=f"gw{a}", align_bytes=64) for a in range(PASSES)]
@@ -126,7 +140,7 @@ def tile_list_tabd_gelu_kernel(tc, tab, w4_words, w4_scales, dw, b, offs, out):
         def gather_words(a):
             nc.vector.tensor_copy(gw[a][:], words[a][:].bitcast(U32).indirect(offsets[:]))
 
-        for a in range(LAST):
+        for a in range(2):
             woven = interleave(nc.scalar.copy, raw[a][:], M, f"bf{a}")
             gather_words(a)
             codes, scales = quantize(woven, M, f"dq{a}")
@@ -137,10 +151,25 @@ def tile_list_tabd_gelu_kernel(tc, tab, w4_words, w4_scales, dw, b, offs, out):
 
         bias = raw[1][:, 0, 0:32]
         nc.vector.transpose(bias, brow[:])
+        gather_words(2)
+        for m in range(MT):
+            base_pass(2, m)
+
+        def change(engine_copy, src, a, m0, count):
+            woven = interleave(engine_copy, src, P * count, f"bf{a}_{m0}")
+            codes, scales = quantize(woven, P * count, f"dq{a}_{m0}")
+            for i in range(count):
+                change_pass(a, m0 + i, codes[:, P * i : P * (i + 1)], scales[:, P * i : P * (i + 1)])
+
+        change(nc.scalar.copy, left[2][:], 2, 0, 2)
         gather_words(LAST)
         for m in range(MT):
-            woven = interleave(nc.vector.tensor_copy, raw_last[m][:], P, f"bf_last{m}")
-            codes, scales = quantize(woven, P, f"dq_last{m}")
             base_pass(LAST, m)
-            change_pass(LAST, m, codes[:], scales[:])
+        change(nc.scalar.copy, left[LAST][:, :, 0:P], LAST, 0, 1)
+        change(nc.vector.tensor_copy, left[LAST][:, :, P : 2 * P], LAST, 1, 1)
+        finish(0)
+        finish(1)
+        for m in (2, 3):
+            for a in (2, LAST):
+                change(nc.vector.tensor_copy, right[a, m][:], a, m, 1)
             finish(m)

@@ -60,14 +60,14 @@ def tile_list_tabd_gelu_kernel(tc, tab, w4_words, w4_scales, dw, b, offs, out):
         )
         nc.sync.dma_start(offsets[:], offs)
         nc.sync.dma_start(stage[0:64, S : S + M].bitcast(I32), w4_scales.rearrange("a r n -> r a n").bitcast(I32))
-        nc.gpsimd.dma_start(brow[0:P:8, :], b.rearrange("(m q i) -> q m i", q=4, i=32))
+        nc.sync.dma_start(brow[0:P:8, :], b.rearrange("(m q i) -> q m i", q=4, i=32))
         load_dw(raw[0], 0, 0, M)
         load_words(0)
         nc.sync.dma_start(w4[:].bitcast(I32), w4_words.rearrange("a p n -> p a n").bitcast(I32))
 
         nc.vector.tensor_copy(picked[:, 0:S], tabs[:].indirect(offsets[:]))
         nc.vector.tensor_copy(stage[0:64, 0:S].bitcast(I32), picked[0:64, 0:S].bitcast(I32))
-        for q in range(4):
+        for q in (0, 2, 1, 3):
             nc.sync.dma_start(
                 planes[32 * q : 32 * q + 4, :, :].bitcast(I32), stage[16 * q : 16 * q + 16, :].bitcast(I32)
             )
@@ -134,8 +134,10 @@ def tile_list_tabd_gelu_kernel(tc, tab, w4_words, w4_scales, dw, b, offs, out):
 
         def finish(m):
             res = keep.tile([P, S], F32, name=f"res{m}")
-            nc.scalar.activation(res[:], acc[m][:], GELU, bias=bias[:, 8 * m : 8 * m + 1])
-            nc.sync.dma_start(out[P * m : P * (m + 1), :], res[:])
+            step = S // 2 if m == MT - 1 else S
+            for c in range(0, S, step):
+                nc.scalar.activation(res[:, c : c + step], acc[m][:, c : c + step], GELU, bias=bias[:, 8 * m : 8 * m + 1])
+                nc.sync.dma_start(out[P * m : P * (m + 1), c : c + step], res[:, c : c + step])
 
         def gather_words(a):
             nc.vector.tensor_copy(gw[a][:], words[a][:].bitcast(U32).indirect(offsets[:]))
@@ -171,5 +173,5 @@ def tile_list_tabd_gelu_kernel(tc, tab, w4_words, w4_scales, dw, b, offs, out):
         finish(1)
         for m in (2, 3):
             for a in (2, LAST):
-                change(nc.vector.tensor_copy, right[a, m][:], a, m, 1)
+                change(nc.scalar.copy if (a, m) == (2, 2) else nc.vector.tensor_copy, right[a, m][:], a, m, 1)
             finish(m)

@@ -31,7 +31,7 @@ def tile_list_tabd_gelu_kernel(tc, tab, w4_words, w4_scales, dw, b, offs, out):
 
         offsets = keep.tile([P, S // 16], U16, name="offsets")
         tabs = keep.tile([P, T], U8, name="tabs", align_bytes=64)
-        picked = late.tile([P, 6 * CHUNK], U8, name="picked", align_bytes=64, offset=0)
+        picked = late.tile([P, 7 * CHUNK], U8, name="picked", align_bytes=64, offset=0)
         stage = keep.tile([P, S + M], U8, name="stage", align_bytes=64)
         planes = keep.tile([P, PASSES, S + M], U8, name="planes", align_bytes=64)
         brow = keep.tile([P, 32], F32, name="brow", align_bytes=64)
@@ -44,7 +44,7 @@ def tile_list_tabd_gelu_kernel(tc, tab, w4_words, w4_scales, dw, b, offs, out):
         warm_out = keep.tile([P, 1], F32, name="warm_out")
         nc.scalar.activation(warm_out[:], warm[:], GELU)
 
-        raw = [keep.tile([P, 4, M], F32, name="raw0", align_bytes=64)]
+        first_right = keep.tile([P, 4, 256], F32, name="first_right", align_bytes=64)
         words = [keep.tile([P, T], I32, name="words0", align_bytes=64)]
         w4 = keep.tile([P, PASSES, 2 * M], U8, name="w4", align_bytes=64)
 
@@ -61,9 +61,9 @@ def tile_list_tabd_gelu_kernel(tc, tab, w4_words, w4_scales, dw, b, offs, out):
         nc.sync.dma_start(offsets[:], offs)
         nc.sync.dma_start(stage[0:64, S : S + M].bitcast(I32), w4_scales.rearrange("a r n -> r a n").bitcast(I32))
         nc.sync.dma_start(brow[0:P:8, :], b.rearrange("(m q i) -> q m i", q=4, i=32))
-        load_dw(raw[0], 0, 0, M)
         load_words(0)
         nc.sync.dma_start(w4[:].bitcast(I32), w4_words.rearrange("a p n -> p a n").bitcast(I32))
+        load_dw(first_right, 0, 256, M)
 
         nc.vector.tensor_copy(picked[:, 0:S], tabs[:].indirect(offsets[:]))
         nc.vector.tensor_copy(stage[0:64, 0:S].bitcast(I32), picked[0:64, 0:S].bitcast(I32))
@@ -72,7 +72,8 @@ def tile_list_tabd_gelu_kernel(tc, tab, w4_words, w4_scales, dw, b, offs, out):
                 planes[32 * q : 32 * q + 4, :, :].bitcast(I32), stage[16 * q : 16 * q + 16, :].bitcast(I32)
             )
 
-        raw.append(late.tile([P, 4, M], F32, name="raw1", align_bytes=64, offset=0))
+        second = late.tile([P, 4, M], F32, name="second", align_bytes=64, offset=0)
+        first_left = late.tile([P, 4, 256], F32, name="first_left", align_bytes=64, offset=6 * CHUNK)
         for a in range(1, PASSES):
             words.append(late.tile([P, T], I32, name=f"words{a}", align_bytes=64, offset=a * CHUNK))
 
@@ -83,8 +84,9 @@ def tile_list_tabd_gelu_kernel(tc, tab, w4_words, w4_scales, dw, b, offs, out):
             load_dw(piece, a, c0, c1)
             return piece
 
-        load_dw(raw[1], 1, 0, M)
+        load_dw(first_left, 0, 0, 256)
         load_words(1)
+        load_dw(second, 1, 0, M)
         load_words(2)
         left = {2: load_piece(2, 0, 256)}
         load_words(LAST)
@@ -96,10 +98,7 @@ def tile_list_tabd_gelu_kernel(tc, tab, w4_words, w4_scales, dw, b, offs, out):
 
         def interleave(engine_copy, src, width, name):
             dst = keep.tile([P, width, 4], BF16, name=name, align_bytes=64)
-            engine_copy(
-                dst[:].rearrange("p (c i) j -> p c j i", i=4),
-                src.rearrange("p j (c i) -> p c j i", i=4),
-            )
+            engine_copy(dst[:], src.rearrange("p j n -> p n j"))
             return dst
 
         def quantize(src, width, name):
@@ -142,27 +141,24 @@ def tile_list_tabd_gelu_kernel(tc, tab, w4_words, w4_scales, dw, b, offs, out):
         def gather_words(a):
             nc.vector.tensor_copy(gw[a][:], words[a][:].bitcast(U32).indirect(offsets[:]))
 
-        for a in range(2):
-            woven = interleave(nc.scalar.copy, raw[a][:], M, f"bf{a}")
-            gather_words(a)
-            codes, scales = quantize(woven, M, f"dq{a}")
-            for m in range(MT):
-                base_pass(a, m)
-            for m in range(MT):
-                change_pass(a, m, codes[:, P * m : P * (m + 1)], scales[:, P * m : P * (m + 1)])
-
-        bias = raw[1][:, 0, 0:32]
-        nc.vector.transpose(bias, brow[:])
-        gather_words(2)
-        for m in range(MT):
-            base_pass(2, m)
-
         def change(engine_copy, src, a, m0, count):
             woven = interleave(engine_copy, src, P * count, f"bf{a}_{m0}")
             codes, scales = quantize(woven, P * count, f"dq{a}_{m0}")
             for i in range(count):
                 change_pass(a, m0 + i, codes[:, P * i : P * (i + 1)], scales[:, P * i : P * (i + 1)])
 
+        for a, lo, hi in ((0, first_left[:], first_right[:]), (1, second[:, :, 0:256], second[:, :, 256:M])):
+            gather_words(a)
+            for m in range(MT):
+                base_pass(a, m)
+            change(nc.vector.tensor_copy, hi, a, 2, 2)
+            change(nc.scalar.copy, lo, a, 0, 2)
+
+        bias = second[:, 0, 0:32]
+        nc.vector.transpose(bias, brow[:])
+        gather_words(2)
+        for m in range(MT):
+            base_pass(2, m)
         change(nc.scalar.copy, left[2][:], 2, 0, 2)
         gather_words(LAST)
         for m in range(MT):

@@ -30,13 +30,15 @@ def tile_list_tabd_gelu_kernel(tc, tab, w4_words, w4_scales, dw, b, offs, out):
         psum = ctx.enter_context(tc.psum_pool(name="psum", bufs=1))
 
         offsets = keep.tile([P, S // 16], U16, name="offsets")
-        tabs = keep.tile([P, T], U8, name="tabs", align_bytes=64)
-        picked = late.tile([P, 7 * CHUNK], U8, name="picked", align_bytes=64, offset=0)
-        stage = keep.tile([P, S + M], U8, name="stage", align_bytes=64)
-        planes = keep.tile([P, PASSES, S + M], U8, name="planes", align_bytes=64)
+        held = late.tile([P, 8 * CHUNK], U8, name="held", align_bytes=64, offset=0)
+        tabs = held[:, 0:T]
+        picked = keep.tile([P, S], U8, name="picked", align_bytes=64)
+        planes = keep.tile([P, PASSES, S], U8, name="planes", align_bytes=64)
+        w4_planes = keep.tile([P, PASSES, M], U8, name="w4_planes", align_bytes=64)
         brow = keep.tile([P, 32], F32, name="brow", align_bytes=64)
         nc.vector.memset(brow[:], 0.0)
         nc.vector.memset(tabs[64:P, :].bitcast(I32), 0)
+        nc.vector.memset(w4_planes[:].bitcast(I32), 0)
         nc.vector.memset(planes[:].bitcast(I32), 0)
 
         warm = keep.tile([P, 1], F32, name="warm")
@@ -44,7 +46,6 @@ def tile_list_tabd_gelu_kernel(tc, tab, w4_words, w4_scales, dw, b, offs, out):
         warm_out = keep.tile([P, 1], F32, name="warm_out")
         nc.scalar.activation(warm_out[:], warm[:], GELU)
 
-        first_right = keep.tile([P, 4, 256], F32, name="first_right", align_bytes=64)
         words = [keep.tile([P, T], I32, name="words0", align_bytes=64)]
         w4 = keep.tile([P, PASSES, 2 * M], U8, name="w4", align_bytes=64)
 
@@ -59,21 +60,23 @@ def tile_list_tabd_gelu_kernel(tc, tab, w4_words, w4_scales, dw, b, offs, out):
             tab[:, 512 * T : 528 * T].rearrange("a (r t) -> r a t", t=T).bitcast(I32),
         )
         nc.sync.dma_start(offsets[:], offs)
-        nc.sync.dma_start(stage[0:64, S : S + M].bitcast(I32), w4_scales.rearrange("a r n -> r a n").bitcast(I32))
-        nc.sync.dma_start(brow[0:P:8, :], b.rearrange("(m q i) -> q m i", q=4, i=32))
         load_words(0)
-        nc.sync.dma_start(w4[:].bitcast(I32), w4_words.rearrange("a p n -> p a n").bitcast(I32))
-        load_dw(first_right, 0, 256, M)
-
-        nc.vector.tensor_copy(picked[:, 0:S], tabs[:].indirect(offsets[:]))
-        nc.vector.tensor_copy(stage[0:64, 0:S].bitcast(I32), picked[0:64, 0:S].bitcast(I32))
         for q in (0, 2, 1, 3):
             nc.sync.dma_start(
-                planes[32 * q : 32 * q + 4, :, :].bitcast(I32), stage[16 * q : 16 * q + 16, :].bitcast(I32)
+                w4_planes[32 * q : 32 * q + 4, :, :].bitcast(I32),
+                w4_scales[:, 4 * q : 4 * q + 4, :].rearrange("a r n -> r a n").bitcast(I32),
+            )
+        nc.sync.dma_start(w4[:].bitcast(I32), w4_words.rearrange("a p n -> p a n").bitcast(I32))
+
+        nc.vector.tensor_copy(picked[:], tabs.indirect(offsets[:]))
+        for q in (0, 2, 1, 3):
+            nc.sync.dma_start(
+                planes[32 * q : 32 * q + 4, :, :].bitcast(I32), picked[16 * q : 16 * q + 16, :].bitcast(I32)
             )
 
         second = late.tile([P, 4, M], F32, name="second", align_bytes=64, offset=0)
         first_left = late.tile([P, 4, 256], F32, name="first_left", align_bytes=64, offset=6 * CHUNK)
+        first_right = late.tile([P, 4, 256], F32, name="first_right", align_bytes=64, offset=7 * CHUNK)
         for a in range(1, PASSES):
             words.append(late.tile([P, T], I32, name=f"words{a}", align_bytes=64, offset=a * CHUNK))
 
@@ -84,6 +87,8 @@ def tile_list_tabd_gelu_kernel(tc, tab, w4_words, w4_scales, dw, b, offs, out):
             load_dw(piece, a, c0, c1)
             return piece
 
+        load_dw(first_right, 0, 256, M)
+        nc.sync.dma_start(brow[0:P:8, :], b.rearrange("(m q i) -> q m i", q=4, i=32))
         load_dw(first_left, 0, 0, 256)
         load_words(1)
         load_dw(second, 1, 0, M)
@@ -113,9 +118,9 @@ def tile_list_tabd_gelu_kernel(tc, tab, w4_words, w4_scales, dw, b, offs, out):
             nc.tensor.matmul_mx(
                 out=acc[m][:],
                 lhsT=w4[:, a, 256 * m : 256 * (m + 1)].bitcast(FP4X4),
-                lhsT_scale=planes[:, a, S + P * m : S + P * (m + 1)],
+                lhsT_scale=w4_planes[:, a, P * m : P * (m + 1)],
                 rhs=gw[a][:].bitcast(FP8X4),
-                rhs_scale=planes[:, a, 0:S],
+                rhs_scale=planes[:, a, :],
                 start=(a == 0),
                 stop=False,
             )
@@ -126,7 +131,7 @@ def tile_list_tabd_gelu_kernel(tc, tab, w4_words, w4_scales, dw, b, offs, out):
                 lhsT=codes.bitcast(FP8X4),
                 lhsT_scale=scales,
                 rhs=gw[a][:].bitcast(FP8X4),
-                rhs_scale=planes[:, a, 0:S],
+                rhs_scale=planes[:, a, :],
                 start=False,
                 stop=(a == LAST),
             )

@@ -30,12 +30,12 @@ def tile_list_tabd_gelu_kernel(tc, tab, w4_words, w4_scales, dw, b, offs, out):
         psum = ctx.enter_context(tc.psum_pool(name="psum", bufs=1))
 
         offsets = keep.tile([P, S // 16], U16, name="offsets")
-        held = late.tile([P, 8 * CHUNK], U8, name="held", align_bytes=64, offset=0)
+        held = late.tile([P, 8 * CHUNK], U8, name="held", align_bytes=256, offset=0)
         tabs = held[:, 0:T]
-        picked = keep.tile([P, S], U8, name="picked", align_bytes=64)
-        planes = keep.tile([P, PASSES, S], U8, name="planes", align_bytes=64)
-        w4_planes = keep.tile([P, PASSES, M], U8, name="w4_planes", align_bytes=64)
-        brow = keep.tile([P, 32], F32, name="brow", align_bytes=64)
+        picked = keep.tile([P, S], U8, name="picked", align_bytes=256)
+        planes = keep.tile([P, PASSES, S], U8, name="planes", align_bytes=256)
+        w4_planes = keep.tile([P, PASSES, M], U8, name="w4_planes", align_bytes=256)
+        brow = keep.tile([P, 32], F32, name="brow", align_bytes=256)
         nc.vector.memset(brow[:], 0.0)
         nc.vector.memset(tabs[64:P, :].bitcast(I32), 0)
         nc.vector.memset(w4_planes[:].bitcast(I32), 0)
@@ -46,8 +46,8 @@ def tile_list_tabd_gelu_kernel(tc, tab, w4_words, w4_scales, dw, b, offs, out):
         warm_out = keep.tile([P, 1], F32, name="warm_out")
         nc.scalar.activation(warm_out[:], warm[:], GELU)
 
-        words = [keep.tile([P, T], I32, name="words0", align_bytes=64)]
-        w4 = keep.tile([P, PASSES, 2 * M], U8, name="w4", align_bytes=64)
+        words = [keep.tile([P, T], I32, name="words0", align_bytes=256)]
+        w4 = keep.tile([P, PASSES, 2 * M], U8, name="w4", align_bytes=256)
 
         def load_dw(dst, a, c0, c1):
             nc.sync.dma_start(dst[:], dw[512 * a : 512 * (a + 1), c0:c1].rearrange("(p j) n -> p j n", j=4))
@@ -74,15 +74,15 @@ def tile_list_tabd_gelu_kernel(tc, tab, w4_words, w4_scales, dw, b, offs, out):
                 planes[32 * q : 32 * q + 4, :, :].bitcast(I32), picked[16 * q : 16 * q + 16, :].bitcast(I32)
             )
 
-        second = late.tile([P, 4, M], F32, name="second", align_bytes=64, offset=0)
-        first_left = late.tile([P, 4, 256], F32, name="first_left", align_bytes=64, offset=6 * CHUNK)
-        first_right = late.tile([P, 4, 256], F32, name="first_right", align_bytes=64, offset=7 * CHUNK)
+        second = late.tile([P, 4, M], F32, name="second", align_bytes=256, offset=0)
+        first_left = late.tile([P, 4, 256], F32, name="first_left", align_bytes=256, offset=6 * CHUNK)
+        first_right = late.tile([P, 4, 256], F32, name="first_right", align_bytes=256, offset=7 * CHUNK)
         for a in range(1, PASSES):
-            words.append(late.tile([P, T], I32, name=f"words{a}", align_bytes=64, offset=a * CHUNK))
+            words.append(late.tile([P, T], I32, name=f"words{a}", align_bytes=256, offset=a * CHUNK))
 
         def load_piece(a, c0, c1):
             piece = late.tile(
-                [P, 4, c1 - c0], F32, name=f"piece{a}_{c0}", align_bytes=64, offset=(a + 2) * CHUNK + 16 * c0
+                [P, 4, c1 - c0], F32, name=f"piece{a}_{c0}", align_bytes=256, offset=(a + 2) * CHUNK + 16 * c0
             )
             load_dw(piece, a, c0, c1)
             return piece
@@ -99,16 +99,16 @@ def tile_list_tabd_gelu_kernel(tc, tab, w4_words, w4_scales, dw, b, offs, out):
         right = {(a, m): load_piece(a, P * m, P * (m + 1)) for m in (2, 3) for a in (2, LAST)}
 
         acc = [psum.tile([P, S], F32, name=f"acc{m}") for m in range(MT)]
-        gw = [keep.tile([P, S], U32, name=f"gw{a}", align_bytes=64) for a in range(PASSES)]
+        gw = [keep.tile([P, S], U32, name=f"gw{a}", align_bytes=256) for a in range(PASSES)]
 
         def interleave(engine_copy, src, width, name):
-            dst = keep.tile([P, width, 4], BF16, name=name, align_bytes=64)
+            dst = keep.tile([P, width, 4], BF16, name=name, align_bytes=256)
             engine_copy(dst[:], src.rearrange("p j n -> p n j"))
             return dst
 
         def quantize(src, width, name):
-            codes = keep.tile([P, width], U32, name=name + "q", align_bytes=64)
-            scales = keep.tile([P, width], U8, name=name + "s", align_bytes=64)
+            codes = keep.tile([P, width], U32, name=name + "q", align_bytes=256)
+            scales = keep.tile([P, width], U8, name=name + "s", align_bytes=256)
             nc.vector.quantize_mx(
                 out=codes[:].bitcast(FP8X4), scales=scales[:], in_=src[:].rearrange("p n j -> p (n j)")
             )
@@ -137,7 +137,7 @@ def tile_list_tabd_gelu_kernel(tc, tab, w4_words, w4_scales, dw, b, offs, out):
             )
 
         def finish(m):
-            res = keep.tile([P, S], F32, name=f"res{m}")
+            res = keep.tile([P, S], F32, name=f"res{m}", align_bytes=256)
             step = S // 2 if m == MT - 1 else S
             for c in range(0, S, step):
                 nc.scalar.activation(res[:, c : c + step], acc[m][:, c : c + step], GELU, bias=bias[:, 8 * m : 8 * m + 1])

@@ -20,6 +20,7 @@ PASSES = K // 512
 MT = M // P
 LAST = PASSES - 1
 CHUNK = 8192
+HALF = S // 2
 
 
 def tile_list_tabd_gelu_kernel(tc, tab, w4_words, w4_scales, dw, b, offs, out):
@@ -30,15 +31,16 @@ def tile_list_tabd_gelu_kernel(tc, tab, w4_words, w4_scales, dw, b, offs, out):
         psum = ctx.enter_context(tc.psum_pool(name="psum", bufs=1))
 
         offsets = keep.tile([P, S // 16], U16, name="offsets")
-        held = late.tile([P, 8 * CHUNK], U8, name="held", align_bytes=256, offset=0)
+        held = late.tile([P, 6 * CHUNK], U8, name="held", align_bytes=256, offset=0)
         tabs = held[:, 0:T]
         picked = keep.tile([P, S], U8, name="picked", align_bytes=256)
         planes = keep.tile([P, PASSES, S], U8, name="planes", align_bytes=256)
         w4_planes = keep.tile([P, PASSES, M], U8, name="w4_planes", align_bytes=256)
         brow = keep.tile([P, 32], F32, name="brow", align_bytes=256)
-        nc.vector.memset(brow[:], 0.0)
-        nc.vector.memset(tabs[64:P, :].bitcast(I32), 0)
         nc.vector.memset(w4_planes[:].bitcast(I32), 0)
+        nc.vector.memset(brow[:], 0.0)
+        nc.vector.memset(tabs[0:32, :].bitcast(I32), 0)
+        nc.vector.memset(tabs[96:P, :].bitcast(I32), 0)
         nc.vector.memset(planes[:].bitcast(I32), 0)
 
         warm = keep.tile([P, 1], F32, name="warm")
@@ -48,6 +50,7 @@ def tile_list_tabd_gelu_kernel(tc, tab, w4_words, w4_scales, dw, b, offs, out):
 
         words = [keep.tile([P, T], I32, name="words0", align_bytes=256)]
         w4 = keep.tile([P, PASSES, 2 * M], U8, name="w4", align_bytes=256)
+        first = keep.tile([P, 4, M], F32, name="first", align_bytes=256)
 
         def load_dw(dst, a, c0, c1):
             nc.sync.dma_start(dst[:], dw[512 * a : 512 * (a + 1), c0:c1].rearrange("(p j) n -> p j n", j=4))
@@ -56,49 +59,47 @@ def tile_list_tabd_gelu_kernel(tc, tab, w4_words, w4_scales, dw, b, offs, out):
             nc.sync.dma_start(words[a][:], tab[a, 0 : 512 * T].rearrange("(p n) -> p n", p=P).bitcast(I32))
 
         nc.sync.dma_start(
-            tabs[0:64, :].bitcast(I32),
+            tabs[32:96, :].bitcast(I32),
             tab[:, 512 * T : 528 * T].rearrange("a (r t) -> r a t", t=T).bitcast(I32),
         )
         nc.sync.dma_start(offsets[:], offs)
         load_words(0)
-        for q in (0, 2, 1, 3):
+        for r in range(4):
             nc.sync.dma_start(
-                w4_planes[32 * q : 32 * q + 4, :, :].bitcast(I32),
-                w4_scales[:, 4 * q : 4 * q + 4, :].rearrange("a r n -> r a n").bitcast(I32),
+                w4_planes[r:P:32, :, :].bitcast(I32),
+                w4_scales[:, r:16:4, :].rearrange("a q n -> q a n").bitcast(I32),
             )
         nc.sync.dma_start(w4[:].bitcast(I32), w4_words.rearrange("a p n -> p a n").bitcast(I32))
+        load_dw(first, 0, 0, M)
 
         nc.vector.tensor_copy(picked[:], tabs.indirect(offsets[:]))
         for q in (0, 2, 1, 3):
             nc.sync.dma_start(
-                planes[32 * q : 32 * q + 4, :, :].bitcast(I32), picked[16 * q : 16 * q + 16, :].bitcast(I32)
+                planes[32 * q : 32 * q + 4, :, :].bitcast(I32), picked[32 + 16 * q : 48 + 16 * q, :].bitcast(I32)
             )
 
         second = late.tile([P, 4, M], F32, name="second", align_bytes=256, offset=0)
-        first_left = late.tile([P, 4, 256], F32, name="first_left", align_bytes=256, offset=6 * CHUNK)
-        first_right = late.tile([P, 4, 256], F32, name="first_right", align_bytes=256, offset=7 * CHUNK)
         for a in range(1, PASSES):
             words.append(late.tile([P, T], I32, name=f"words{a}", align_bytes=256, offset=a * CHUNK))
 
+        def place(a, c0):
+            return (a + 2) * CHUNK + 16 * c0
+
         def load_piece(a, c0, c1):
-            piece = late.tile(
-                [P, 4, c1 - c0], F32, name=f"piece{a}_{c0}", align_bytes=256, offset=(a + 2) * CHUNK + 16 * c0
-            )
+            piece = late.tile([P, 4, c1 - c0], F32, name=f"piece{a}_{c0}", align_bytes=256, offset=place(a, c0))
             load_dw(piece, a, c0, c1)
             return piece
 
-        load_dw(first_right, 0, 256, M)
         nc.sync.dma_start(brow[0:P:8, :], b.rearrange("(m q i) -> q m i", q=4, i=32))
-        load_dw(first_left, 0, 0, 256)
         load_words(1)
         load_dw(second, 1, 0, M)
         load_words(2)
-        left = {2: load_piece(2, 0, 256)}
         load_words(LAST)
-        left[LAST] = load_piece(LAST, 0, 256)
+        left = {a: load_piece(a, 0, 256) for a in (2, LAST)}
         right = {(a, m): load_piece(a, P * m, P * (m + 1)) for m in (2, 3) for a in (2, LAST)}
 
-        acc = [psum.tile([P, S], F32, name=f"acc{m}") for m in range(MT)]
+        banks = {m: [(psum.tile([P, S], F32, name=f"acc{m}"), 0, S)] for m in range(MT - 1)}
+        banks[MT - 1] = [(psum.tile([P, HALF], F32, name=f"acc_last{h}"), HALF * h, HALF * (h + 1)) for h in range(2)]
         gw = [keep.tile([P, S], U32, name=f"gw{a}", align_bytes=256) for a in range(PASSES)]
 
         def interleave(engine_copy, src, width, name):
@@ -106,73 +107,79 @@ def tile_list_tabd_gelu_kernel(tc, tab, w4_words, w4_scales, dw, b, offs, out):
             engine_copy(dst[:], src.rearrange("p j n -> p n j"))
             return dst
 
-        def quantize(src, width, name):
-            codes = keep.tile([P, width], U32, name=name + "q", align_bytes=256)
+        def quantize(src, width, name, offset=None):
+            if offset is None:
+                codes = keep.tile([P, width], U32, name=name + "q", align_bytes=256)
+            else:
+                codes = late.tile([P, width], U32, name=name + "q", align_bytes=256, offset=offset)
             scales = keep.tile([P, width], U8, name=name + "s", align_bytes=256)
             nc.vector.quantize_mx(
                 out=codes[:].bitcast(FP8X4), scales=scales[:], in_=src[:].rearrange("p n j -> p (n j)")
             )
             return codes, scales
 
-        def base_pass(a, m):
-            nc.tensor.matmul_mx(
-                out=acc[m][:],
-                lhsT=w4[:, a, 256 * m : 256 * (m + 1)].bitcast(FP4X4),
-                lhsT_scale=w4_planes[:, a, P * m : P * (m + 1)],
-                rhs=gw[a][:].bitcast(FP8X4),
-                rhs_scale=planes[:, a, :],
-                start=(a == 0),
-                stop=False,
-            )
+        def one_pass(a, m, lhsT, lhsT_scale, start, stop):
+            for acc, c0, c1 in banks[m]:
+                nc.tensor.matmul_mx(
+                    out=acc[:],
+                    lhsT=lhsT,
+                    lhsT_scale=lhsT_scale,
+                    rhs=gw[a][:, c0:c1].bitcast(FP8X4),
+                    rhs_scale=planes[:, a, c0:c1],
+                    start=start,
+                    stop=stop,
+                )
 
-        def change_pass(a, m, codes, scales):
-            nc.tensor.matmul_mx(
-                out=acc[m][:],
-                lhsT=codes.bitcast(FP8X4),
-                lhsT_scale=scales,
-                rhs=gw[a][:].bitcast(FP8X4),
-                rhs_scale=planes[:, a, :],
-                start=False,
-                stop=(a == LAST),
-            )
+        def base_passes(a):
+            for m in range(MT):
+                one_pass(
+                    a, m, w4[:, a, 256 * m : 256 * (m + 1)].bitcast(FP4X4), w4_planes[:, a, P * m : P * (m + 1)],
+                    a == 0, False,
+                )
 
         def finish(m):
             res = keep.tile([P, S], F32, name=f"res{m}", align_bytes=256)
-            step = S // 2 if m == MT - 1 else S
-            for c in range(0, S, step):
-                nc.scalar.activation(res[:, c : c + step], acc[m][:, c : c + step], GELU, bias=bias[:, 8 * m : 8 * m + 1])
-                nc.sync.dma_start(out[P * m : P * (m + 1), c : c + step], res[:, c : c + step])
+            for acc, c0, c1 in banks[m]:
+                nc.scalar.activation(res[:, c0:c1], acc[:], GELU, bias=bias[:, 8 * m : 8 * m + 1])
+                nc.sync.dma_start(out[P * m : P * (m + 1), c0:c1], res[:, c0:c1])
 
         def gather_words(a):
             nc.vector.tensor_copy(gw[a][:], words[a][:].bitcast(U32).indirect(offsets[:]))
 
-        def change(engine_copy, src, a, m0, count):
-            woven = interleave(engine_copy, src, P * count, f"bf{a}_{m0}")
-            codes, scales = quantize(woven, P * count, f"dq{a}_{m0}")
+        def change_passes(woven, a, m0, count, offset=None):
+            codes, scales = quantize(woven, P * count, f"dq{a}_{m0}", offset)
             for i in range(count):
-                change_pass(a, m0 + i, codes[:, P * i : P * (i + 1)], scales[:, P * i : P * (i + 1)])
+                one_pass(
+                    a, m0 + i, codes[:, P * i : P * (i + 1)].bitcast(FP8X4), scales[:, P * i : P * (i + 1)],
+                    False, a == LAST,
+                )
 
-        for a, lo, hi in ((0, first_left[:], first_right[:]), (1, second[:, :, 0:256], second[:, :, 256:M])):
+        def change(engine_copy, src, a, m0, count):
+            change_passes(interleave(engine_copy, src, P * count, f"bf{a}_{m0}"), a, m0, count)
+
+        for a, whole in ((0, first), (1, second)):
             gather_words(a)
-            for m in range(MT):
-                base_pass(a, m)
-            change(nc.vector.tensor_copy, hi, a, 2, 2)
-            change(nc.scalar.copy, lo, a, 0, 2)
+            base_passes(a)
+            change(nc.vector.tensor_copy, whole[:, :, 256:M], a, 2, 2)
+            change(nc.scalar.copy, whole[:, :, 0:256], a, 0, 2)
 
         bias = second[:, 0, 0:32]
         nc.vector.transpose(bias, brow[:])
-        gather_words(2)
-        for m in range(MT):
-            base_pass(2, m)
-        change(nc.scalar.copy, left[2][:], 2, 0, 2)
-        gather_words(LAST)
-        for m in range(MT):
-            base_pass(LAST, m)
-        change(nc.scalar.copy, left[LAST][:, :, 0:P], LAST, 0, 1)
+        for a in (2, LAST):
+            gather_words(a)
+            base_passes(a)
+        change(nc.vector.tensor_copy, left[2][:, :, P : 2 * P], 2, 1, 1)
+        change(nc.scalar.copy, left[2][:, :, 0:P], 2, 0, 1)
+
         change(nc.vector.tensor_copy, left[LAST][:, :, P : 2 * P], LAST, 1, 1)
-        finish(0)
+        change(nc.scalar.copy, left[LAST][:, :, 0:P], LAST, 0, 1)
+        change(nc.scalar.copy, right[2, 2][:], 2, 2, 1)
         finish(1)
-        for m in (2, 3):
-            for a in (2, LAST):
-                change(nc.scalar.copy if (a, m) == (2, 2) else nc.vector.tensor_copy, right[a, m][:], a, m, 1)
-            finish(m)
+        finish(0)
+        change(nc.vector.tensor_copy, right[LAST, 2][:], LAST, 2, 1)
+        finish(2)
+        ahead = interleave(nc.vector.tensor_copy, right[2, 3][:], P, "bf2_3")
+        final = interleave(nc.vector.tensor_copy, right[LAST, 3][:], P, "bf3_3")
+        change_passes(ahead, 2, 3, 1, place(LAST, P * 3))
+        change_passes(final, LAST, 3, 1)
+        finish(3)

@@ -17,10 +17,11 @@ GELU = mybir.ActivationFunctionType.Gelu_apprx_tanh
 
 P = 128
 PASSES = K // 512
-MT = M // P
+TILES = M // P
 LAST = PASSES - 1
-CHUNK = 8192
+CHUNK = 4 * T
 HALF = S // 2
+ROW0 = 32
 
 
 def tile_list_tabd_gelu_kernel(tc, tab, w4_words, w4_scales, dw, b, offs, out):
@@ -32,15 +33,15 @@ def tile_list_tabd_gelu_kernel(tc, tab, w4_words, w4_scales, dw, b, offs, out):
 
         offsets = keep.tile([P, S // 16], U16, name="offsets")
         held = late.tile([P, 6 * CHUNK], U8, name="held", align_bytes=256, offset=0)
-        tabs = held[:, 0:T]
+        window = held[:, 0:T]
         picked = keep.tile([P, S], U8, name="picked", align_bytes=256)
         planes = keep.tile([P, PASSES, S], U8, name="planes", align_bytes=256)
         w4_planes = keep.tile([P, PASSES, M], U8, name="w4_planes", align_bytes=256)
-        brow = keep.tile([P, 32], F32, name="brow", align_bytes=256)
+        bias_rows = keep.tile([P, 32], F32, name="bias_rows", align_bytes=256)
         nc.vector.memset(w4_planes[:].bitcast(I32), 0)
-        nc.vector.memset(brow[:], 0.0)
-        nc.vector.memset(tabs[0:32, :].bitcast(I32), 0)
-        nc.vector.memset(tabs[96:P, :].bitcast(I32), 0)
+        nc.vector.memset(bias_rows[:], 0.0)
+        nc.vector.memset(window[0:ROW0, :].bitcast(I32), 0)
+        nc.vector.memset(window[ROW0 + 64 : P, :].bitcast(I32), 0)
         nc.vector.memset(planes[:].bitcast(I32), 0)
 
         warm = keep.tile([P, 1], F32, name="warm")
@@ -48,75 +49,56 @@ def tile_list_tabd_gelu_kernel(tc, tab, w4_words, w4_scales, dw, b, offs, out):
         warm_out = keep.tile([P, 1], F32, name="warm_out")
         nc.scalar.activation(warm_out[:], warm[:], GELU)
 
-        words = [keep.tile([P, T], I32, name="words0", align_bytes=256)]
-        w4 = keep.tile([P, PASSES, 2 * M], U8, name="w4", align_bytes=256)
-        first = keep.tile([P, 4, M], F32, name="first", align_bytes=256)
+        def place(a, c0):
+            return {1: 0, 2: 4, LAST: 5}[a] * CHUNK + 16 * c0
 
-        def load_dw(dst, a, c0, c1):
-            nc.sync.dma_start(dst[:], dw[512 * a : 512 * (a + 1), c0:c1].rearrange("(p j) n -> p j n", j=4))
+        def load_dw(a, c0, c1, pool, **where):
+            piece = pool.tile([P, 4, c1 - c0], F32, name=f"dw{a}_{c0}", align_bytes=256, **where)
+            nc.sync.dma_start(piece[:], dw[512 * a : 512 * (a + 1), c0:c1].rearrange("(p j) n -> p j n", j=4))
+            return piece
 
-        def load_words(a):
-            nc.sync.dma_start(words[a][:], tab[a, 0 : 512 * T].rearrange("(p n) -> p n", p=P).bitcast(I32))
+        def load_held_dw(a, c0, c1):
+            return load_dw(a, c0, c1, late, offset=place(a, c0))
+
+        def load_words(a, pool, **where):
+            tile = pool.tile([P, T], I32, name=f"words{a}", align_bytes=256, **where)
+            nc.sync.dma_start(tile[:], tab[a, 0 : 512 * T].rearrange("(p n) -> p n", p=P).bitcast(I32))
+            return tile
 
         nc.sync.dma_start(
-            tabs[32:96, :].bitcast(I32),
-            tab[:, 512 * T : 528 * T].rearrange("a (r t) -> r a t", t=T).bitcast(I32),
+            window[ROW0 : ROW0 + 64, :].bitcast(I32),
+            tab[:, 512 * T : 528 * T].rearrange("a (g t) -> g a t", t=T).bitcast(I32),
         )
         nc.sync.dma_start(offsets[:], offs)
-        load_words(0)
+        words = [load_words(0, keep)]
         for r in range(4):
             nc.sync.dma_start(
                 w4_planes[r:P:32, :, :].bitcast(I32),
                 w4_scales[:, r:16:4, :].rearrange("a q n -> q a n").bitcast(I32),
             )
+        w4 = keep.tile([P, PASSES, 2 * M], U8, name="w4", align_bytes=256)
         nc.sync.dma_start(w4[:].bitcast(I32), w4_words.rearrange("a p n -> p a n").bitcast(I32))
-        load_dw(first, 0, 0, M)
+        whole = load_dw(0, 0, M, keep)
 
-        nc.vector.tensor_copy(picked[:], tabs.indirect(offsets[:]))
+        nc.vector.tensor_copy(picked[:], window.indirect(offsets[:]))
         for q in (0, 2, 1, 3):
             nc.sync.dma_start(
-                planes[32 * q : 32 * q + 4, :, :].bitcast(I32), picked[32 + 16 * q : 48 + 16 * q, :].bitcast(I32)
+                planes[32 * q : 32 * q + 4, :, :].bitcast(I32),
+                picked[ROW0 + 16 * q : ROW0 + 16 * (q + 1), :].bitcast(I32),
             )
 
-        second = late.tile([P, 4, M], F32, name="second", align_bytes=256, offset=0)
-        for a in range(1, PASSES):
-            words.append(late.tile([P, T], I32, name=f"words{a}", align_bytes=256, offset=a * CHUNK))
+        nc.sync.dma_start(bias_rows[0:P:8, :], b.rearrange("(m q i) -> q m i", q=4, i=32))
+        words.append(load_words(1, late, offset=CHUNK))
+        second = load_held_dw(1, 0, M)
+        words.extend(load_words(a, late, offset=a * CHUNK) for a in (2, LAST))
+        left = {a: load_held_dw(a, 0, 2 * P) for a in (2, LAST)}
+        right = {(a, m): load_held_dw(a, P * m, P * (m + 1)) for m in (2, 3) for a in (2, LAST)}
 
-        def place(a, c0):
-            return (a + 2) * CHUNK + 16 * c0
-
-        def load_piece(a, c0, c1):
-            piece = late.tile([P, 4, c1 - c0], F32, name=f"piece{a}_{c0}", align_bytes=256, offset=place(a, c0))
-            load_dw(piece, a, c0, c1)
-            return piece
-
-        nc.sync.dma_start(brow[0:P:8, :], b.rearrange("(m q i) -> q m i", q=4, i=32))
-        load_words(1)
-        load_dw(second, 1, 0, M)
-        load_words(2)
-        load_words(LAST)
-        left = {a: load_piece(a, 0, 256) for a in (2, LAST)}
-        right = {(a, m): load_piece(a, P * m, P * (m + 1)) for m in (2, 3) for a in (2, LAST)}
-
-        banks = {m: [(psum.tile([P, S], F32, name=f"acc{m}"), 0, S)] for m in range(MT - 1)}
-        banks[MT - 1] = [(psum.tile([P, HALF], F32, name=f"acc_last{h}"), HALF * h, HALF * (h + 1)) for h in range(2)]
-        gw = [keep.tile([P, S], U32, name=f"gw{a}", align_bytes=256) for a in range(PASSES)]
-
-        def interleave(engine_copy, src, width, name):
-            dst = keep.tile([P, width, 4], BF16, name=name, align_bytes=256)
-            engine_copy(dst[:], src.rearrange("p j n -> p n j"))
-            return dst
-
-        def quantize(src, width, name, offset=None):
-            if offset is None:
-                codes = keep.tile([P, width], U32, name=name + "q", align_bytes=256)
-            else:
-                codes = late.tile([P, width], U32, name=name + "q", align_bytes=256, offset=offset)
-            scales = keep.tile([P, width], U8, name=name + "s", align_bytes=256)
-            nc.vector.quantize_mx(
-                out=codes[:].bitcast(FP8X4), scales=scales[:], in_=src[:].rearrange("p n j -> p (n j)")
-            )
-            return codes, scales
+        banks = {m: [(psum.tile([P, S], F32, name=f"acc{m}"), 0, S)] for m in range(TILES - 1)}
+        banks[TILES - 1] = [
+            (psum.tile([P, HALF], F32, name=f"acc_last{h}"), HALF * h, HALF * (h + 1)) for h in range(2)
+        ]
+        gathered = [keep.tile([P, S], U32, name=f"gathered{a}", align_bytes=256) for a in range(PASSES)]
 
         def one_pass(a, m, lhsT, lhsT_scale, start, stop):
             for acc, c0, c1 in banks[m]:
@@ -124,62 +106,71 @@ def tile_list_tabd_gelu_kernel(tc, tab, w4_words, w4_scales, dw, b, offs, out):
                     out=acc[:],
                     lhsT=lhsT,
                     lhsT_scale=lhsT_scale,
-                    rhs=gw[a][:, c0:c1].bitcast(FP8X4),
+                    rhs=gathered[a][:, c0:c1].bitcast(FP8X4),
                     rhs_scale=planes[:, a, c0:c1],
                     start=start,
                     stop=stop,
                 )
 
-        def base_passes(a):
-            for m in range(MT):
+        def w4_passes(a):
+            nc.vector.tensor_copy(gathered[a][:], words[a][:].bitcast(U32).indirect(offsets[:]))
+            for m in range(TILES):
                 one_pass(
-                    a, m, w4[:, a, 256 * m : 256 * (m + 1)].bitcast(FP4X4), w4_planes[:, a, P * m : P * (m + 1)],
+                    a, m, w4[:, a, 2 * P * m : 2 * P * (m + 1)].bitcast(FP4X4), w4_planes[:, a, P * m : P * (m + 1)],
                     a == 0, False,
                 )
 
-        def finish(m):
-            res = keep.tile([P, S], F32, name=f"res{m}", align_bytes=256)
+        def weave(src, a, m0, copies):
+            width = src.shape[2]
+            share = width // len(copies)
+            dst = keep.tile([P, width, 4], BF16, name=f"woven{a}_{m0}", align_bytes=256)
+            for n, copy in enumerate(copies):
+                cols = slice(share * n, share * (n + 1))
+                copy(
+                    dst[:, cols, :].rearrange("p (c i) j -> p c j i", i=2),
+                    src[:, :, cols].rearrange("p j (c i) -> p c j i", i=2),
+                )
+            return dst
+
+        def dw_passes(woven, a, m0, stop, pool=keep, **where):
+            width = woven.shape[1]
+            codes = pool.tile([P, width], U32, name=f"codes{a}_{m0}", align_bytes=256, **where)
+            scales = keep.tile([P, width], U8, name=f"scales{a}_{m0}", align_bytes=256)
+            nc.vector.quantize_mx(
+                out=codes[:].bitcast(FP8X4), scales=scales[:], in_=woven[:].rearrange("p n j -> p (n j)")
+            )
+            for i in range(width // P):
+                cols = slice(P * i, P * (i + 1))
+                one_pass(a, m0 + i, codes[:, cols].bitcast(FP8X4), scales[:, cols], False, stop)
+
+        def change(src, a, m0, copies):
+            dw_passes(weave(src, a, m0, copies), a, m0, a == LAST)
+
+        def finish(m, pool=keep, **where):
+            res = pool.tile([P, S], F32, name=f"res{m}", align_bytes=256, **where)
             for acc, c0, c1 in banks[m]:
                 nc.scalar.activation(res[:, c0:c1], acc[:], GELU, bias=bias[:, 8 * m : 8 * m + 1])
                 nc.sync.dma_start(out[P * m : P * (m + 1), c0:c1], res[:, c0:c1])
 
-        def gather_words(a):
-            nc.vector.tensor_copy(gw[a][:], words[a][:].bitcast(U32).indirect(offsets[:]))
-
-        def change_passes(woven, a, m0, count, offset=None):
-            codes, scales = quantize(woven, P * count, f"dq{a}_{m0}", offset)
-            for i in range(count):
-                one_pass(
-                    a, m0 + i, codes[:, P * i : P * (i + 1)].bitcast(FP8X4), scales[:, P * i : P * (i + 1)],
-                    False, a == LAST,
-                )
-
-        def change(engine_copy, src, a, m0, count):
-            change_passes(interleave(engine_copy, src, P * count, f"bf{a}_{m0}"), a, m0, count)
-
-        for a, whole in ((0, first), (1, second)):
-            gather_words(a)
-            base_passes(a)
-            change(nc.vector.tensor_copy, whole[:, :, 256:M], a, 2, 2)
-            change(nc.scalar.copy, whole[:, :, 0:256], a, 0, 2)
-
+        vector, scalar = nc.vector.tensor_copy, nc.scalar.copy
+        for a, tile in ((0, whole), (1, second)):
+            w4_passes(a)
+            change(tile[:, :, 2 * P : M], a, 2, (vector,))
+            change(tile[:, :, 0 : 2 * P], a, 0, (scalar,))
         bias = second[:, 0, 0:32]
-        nc.vector.transpose(bias, brow[:])
+        nc.vector.transpose(bias, bias_rows[:])
         for a in (2, LAST):
-            gather_words(a)
-            base_passes(a)
-        change(nc.vector.tensor_copy, left[2][:, :, P : 2 * P], 2, 1, 1)
-        change(nc.scalar.copy, left[2][:, :, 0:P], 2, 0, 1)
-
-        change(nc.vector.tensor_copy, left[LAST][:, :, P : 2 * P], LAST, 1, 1)
-        change(nc.scalar.copy, left[LAST][:, :, 0:P], LAST, 0, 1)
-        change(nc.scalar.copy, right[2, 2][:], 2, 2, 1)
+            w4_passes(a)
+        for a in (2, LAST):
+            change(left[a][:, :, P : 2 * P], a, 1, (vector,))
+            change(left[a][:, :, 0:P], a, 0, (scalar,))
+        change(right[2, 2][:], 2, 2, (scalar,))
         finish(1)
         finish(0)
-        change(nc.vector.tensor_copy, right[LAST, 2][:], LAST, 2, 1)
+        change(right[LAST, 2][:], LAST, 2, (vector,))
         finish(2)
-        ahead = interleave(nc.vector.tensor_copy, right[2, 3][:], P, "bf2_3")
-        final = interleave(nc.vector.tensor_copy, right[LAST, 3][:], P, "bf3_3")
-        change_passes(ahead, 2, 3, 1, place(LAST, P * 3))
-        change_passes(final, LAST, 3, 1)
+        ahead = weave(right[2, 3][:], 2, 3, (vector,))
+        final = weave(right[LAST, 3][:], LAST, 3, (vector,))
+        dw_passes(ahead, 2, 3, False, late, offset=place(LAST, 3 * P))
+        dw_passes(final, LAST, 3, True)
         finish(3)

@@ -22,6 +22,7 @@ LAST = PASSES - 1
 CHUNK = 4 * T
 HALF = S // 2
 ROW0 = 32
+LATE = 2
 
 
 def tile_list_tabd_gelu_kernel(tc, tab, w4_words, w4_scales, dw, b, offs, out):
@@ -32,7 +33,7 @@ def tile_list_tabd_gelu_kernel(tc, tab, w4_words, w4_scales, dw, b, offs, out):
         psum = ctx.enter_context(tc.psum_pool(name="psum", bufs=1))
 
         offsets = keep.tile([P, S // 16], U16, name="offsets")
-        held = late.tile([P, 6 * CHUNK], U8, name="held", align_bytes=256, offset=0)
+        held = late.tile([P, 7 * CHUNK], U8, name="held", align_bytes=256, offset=0)
         window = held[:, 0:T]
         picked = keep.tile([P, S], U8, name="picked", align_bytes=256)
         planes = keep.tile([P, PASSES, S], U8, name="planes", align_bytes=256)
@@ -76,8 +77,18 @@ def tile_list_tabd_gelu_kernel(tc, tab, w4_words, w4_scales, dw, b, offs, out):
                 w4_planes[r:P:32, :, :].bitcast(I32),
                 w4_scales[:, r:16:4, :].rearrange("a q n -> q a n").bitcast(I32),
             )
-        w4 = keep.tile([P, PASSES, 2 * M], U8, name="w4", align_bytes=256)
-        nc.sync.dma_start(w4[:].bitcast(I32), w4_words.rearrange("a p n -> p a n").bitcast(I32))
+        w4 = {}
+
+        def load_w4(a0, a1, m0, m1, pool, **where):
+            tile = pool.tile([P, a1 - a0, 2 * P * (m1 - m0)], U8, name=f"w4_{a0}_{m0}", align_bytes=256, **where)
+            rows = w4_words[a0:a1, :, 2 * P * m0 : 2 * P * m1].rearrange("a p n -> p a n")
+            nc.sync.dma_start(tile[:].bitcast(I32), rows.bitcast(I32))
+            for a in range(a0, a1):
+                for m in range(m0, m1):
+                    w4[a, m] = tile[:, a - a0, 2 * P * (m - m0) : 2 * P * (m - m0 + 1)]
+
+        load_w4(0, LATE, 0, TILES, keep)
+        load_w4(LATE, PASSES, 0, 3, keep)
         whole = load_dw(0, 0, M, keep)
 
         nc.vector.tensor_copy(picked[:], window.indirect(offsets[:]))
@@ -90,9 +101,12 @@ def tile_list_tabd_gelu_kernel(tc, tab, w4_words, w4_scales, dw, b, offs, out):
         nc.sync.dma_start(bias_rows[0:P:8, :], b.rearrange("(m q i) -> q m i", q=4, i=32))
         words.append(load_words(1, late, offset=CHUNK))
         second = load_held_dw(1, 0, M)
-        words.extend(load_words(a, late, offset=a * CHUNK) for a in (2, LAST))
+        words.append(load_words(2, late, offset=2 * CHUNK))
+        words.append(load_words(LAST, late, offset=LAST * CHUNK))
         left = {a: load_held_dw(a, 0, 2 * P) for a in (2, LAST)}
-        right = {(a, m): load_held_dw(a, P * m, P * (m + 1)) for m in (2, 3) for a in (2, LAST)}
+        right = {(a, m): load_held_dw(a, P * m, P * (m + 1)) for a, m in ((2, 2), (LAST, 2), (2, 3))}
+        ends = [load_held_dw(LAST, c, c + P // 2) for c in (3 * P, 3 * P + P // 2)]
+        load_w4(LATE, PASSES, 3, TILES, late, offset=6 * CHUNK + 2048)
 
         banks = {m: [(psum.tile([P, S], F32, name=f"acc{m}"), 0, S)] for m in range(TILES - 1)}
         banks[TILES - 1] = [
@@ -100,8 +114,8 @@ def tile_list_tabd_gelu_kernel(tc, tab, w4_words, w4_scales, dw, b, offs, out):
         ]
         gathered = [keep.tile([P, S], U32, name=f"gathered{a}", align_bytes=256) for a in range(PASSES)]
 
-        def one_pass(a, m, lhsT, lhsT_scale, start, stop):
-            for acc, c0, c1 in banks[m]:
+        def one_pass(a, m, lhsT, lhsT_scale, start, stop, which=slice(None)):
+            for acc, c0, c1 in banks[m][which]:
                 nc.tensor.matmul_mx(
                     out=acc[:],
                     lhsT=lhsT,
@@ -112,13 +126,13 @@ def tile_list_tabd_gelu_kernel(tc, tab, w4_words, w4_scales, dw, b, offs, out):
                     stop=stop,
                 )
 
+        def w4_pass(a, m, stop=False, which=slice(None)):
+            one_pass(a, m, w4[a, m].bitcast(FP4X4), w4_planes[:, a, P * m : P * (m + 1)], a == 0, stop, which)
+
         def w4_passes(a):
             nc.vector.tensor_copy(gathered[a][:], words[a][:].bitcast(U32).indirect(offsets[:]))
-            for m in range(TILES):
-                one_pass(
-                    a, m, w4[:, a, 2 * P * m : 2 * P * (m + 1)].bitcast(FP4X4), w4_planes[:, a, P * m : P * (m + 1)],
-                    a == 0, False,
-                )
+            for m in range(TILES if a < LATE else 3):
+                w4_pass(a, m)
 
         def weave(src, a, m0, copies):
             width = src.shape[2]
@@ -132,14 +146,18 @@ def tile_list_tabd_gelu_kernel(tc, tab, w4_words, w4_scales, dw, b, offs, out):
                 )
             return dst
 
-        def dw_passes(woven, a, m0, stop, pool=keep, **where):
+        def quantise(woven, a, m0, pool=keep, **where):
             width = woven.shape[1]
             codes = pool.tile([P, width], U32, name=f"codes{a}_{m0}", align_bytes=256, **where)
             scales = keep.tile([P, width], U8, name=f"scales{a}_{m0}", align_bytes=256)
             nc.vector.quantize_mx(
                 out=codes[:].bitcast(FP8X4), scales=scales[:], in_=woven[:].rearrange("p n j -> p (n j)")
             )
-            for i in range(width // P):
+            return codes, scales
+
+        def dw_passes(woven, a, m0, stop):
+            codes, scales = quantise(woven, a, m0)
+            for i in range(woven.shape[1] // P):
                 cols = slice(P * i, P * (i + 1))
                 one_pass(a, m0 + i, codes[:, cols].bitcast(FP8X4), scales[:, cols], False, stop)
 
@@ -170,7 +188,18 @@ def tile_list_tabd_gelu_kernel(tc, tab, w4_words, w4_scales, dw, b, offs, out):
         change(right[LAST, 2][:], LAST, 2, (vector,))
         finish(2)
         ahead = weave(right[2, 3][:], 2, 3, (vector,))
-        final = weave(right[LAST, 3][:], LAST, 3, (vector,))
-        dw_passes(ahead, 2, 3, False, late, offset=place(LAST, 3 * P))
-        dw_passes(final, LAST, 3, True)
+        final = keep.tile([P, P, 4], BF16, name="woven_final", align_bytes=256)
+        for n, piece in enumerate(ends):
+            vector(
+                final[:, P // 2 * n : P // 2 * (n + 1), :].rearrange("p (c i) j -> p c j i", i=2),
+                piece[:].rearrange("p j (c i) -> p c j i", i=2),
+            )
+        ahead_codes, ahead_scales = quantise(ahead, 2, 3, late, offset=place(LAST, 3 * P + P // 2))
+        final_codes, final_scales = quantise(final, LAST, 3)
+        for a in range(LATE, PASSES):
+            w4_pass(a, 3)
+        for h in range(2):
+            bank = slice(h, h + 1)
+            one_pass(2, 3, ahead_codes[:].bitcast(FP8X4), ahead_scales[:], False, False, bank)
+            one_pass(LAST, 3, final_codes[:].bitcast(FP8X4), final_scales[:], False, True, bank)
         finish(3)

@@ -22,7 +22,6 @@ LAST = PASSES - 1
 CHUNK = 4 * T
 HALF = S // 2
 ROW0 = 32
-LATE = 2
 
 
 def tile_list_tabd_gelu_kernel(tc, tab, w4_words, w4_scales, dw, b, offs, out):
@@ -87,8 +86,7 @@ def tile_list_tabd_gelu_kernel(tc, tab, w4_words, w4_scales, dw, b, offs, out):
                 for m in range(m0, m1):
                     w4[a, m] = tile[:, a - a0, 2 * P * (m - m0) : 2 * P * (m - m0 + 1)]
 
-        load_w4(0, LATE, 0, TILES, keep)
-        load_w4(LATE, PASSES, 0, 3, keep)
+        load_w4(0, PASSES, 0, TILES, keep)
         whole = load_dw(0, 0, M, keep)
 
         nc.vector.tensor_copy(picked[:], window.indirect(offsets[:]))
@@ -106,7 +104,6 @@ def tile_list_tabd_gelu_kernel(tc, tab, w4_words, w4_scales, dw, b, offs, out):
         left = {a: load_held_dw(a, 0, 2 * P) for a in (2, LAST)}
         right = {(a, m): load_held_dw(a, P * m, P * (m + 1)) for a, m in ((2, 2), (LAST, 2), (2, 3))}
         ends = [load_held_dw(LAST, c, c + P // 2) for c in (3 * P, 3 * P + P // 2)]
-        load_w4(LATE, PASSES, 3, TILES, late, offset=6 * CHUNK + 2048)
 
         banks = {m: [(psum.tile([P, S], F32, name=f"acc{m}"), 0, S)] for m in range(TILES - 1)}
         banks[TILES - 1] = [
@@ -131,7 +128,7 @@ def tile_list_tabd_gelu_kernel(tc, tab, w4_words, w4_scales, dw, b, offs, out):
 
         def w4_passes(a):
             nc.vector.tensor_copy(gathered[a][:], words[a][:].bitcast(U32).indirect(offsets[:]))
-            for m in range(TILES if a < LATE else 3):
+            for m in range(TILES):
                 w4_pass(a, m)
 
         def weave(src, a, m0, copies):
@@ -196,8 +193,6 @@ def tile_list_tabd_gelu_kernel(tc, tab, w4_words, w4_scales, dw, b, offs, out):
             )
         ahead_codes, ahead_scales = quantise(ahead, 2, 3, late, offset=place(LAST, 3 * P + P // 2))
         final_codes, final_scales = quantise(final, LAST, 3)
-        for a in range(LATE, PASSES):
-            w4_pass(a, 3)
         for h in range(2):
             bank = slice(h, h + 1)
             one_pass(2, 3, ahead_codes[:].bitcast(FP8X4), ahead_scales[:], False, False, bank)

@@ -86,7 +86,8 @@ def tile_list_tabd_gelu_kernel(tc, tab, w4_words, w4_scales, dw, b, offs, out):
                 for m in range(m0, m1):
                     w4[a, m] = tile[:, a - a0, 2 * P * (m - m0) : 2 * P * (m - m0 + 1)]
 
-        load_w4(0, PASSES, 0, TILES, keep)
+        load_w4(0, 2, 0, TILES, keep)
+        load_w4(2, PASSES, 0, TILES, keep)
         whole = load_dw(0, 0, M, keep)
 
         nc.vector.tensor_copy(picked[:], window.indirect(offsets[:]))
@@ -96,7 +97,9 @@ def tile_list_tabd_gelu_kernel(tc, tab, w4_words, w4_scales, dw, b, offs, out):
                 picked[ROW0 + 16 * q : ROW0 + 16 * (q + 1), :].bitcast(I32),
             )
 
-        nc.sync.dma_start(bias_rows[0:P:8, :], b.rearrange("(m q i) -> q m i", q=4, i=32))
+        for h in range(2):
+            rows = b.rearrange("(m q i) -> q m i", q=4, i=32)[2 * h : 2 * h + 2]
+            nc.sync.dma_start(bias_rows[64 * h : 64 * (h + 1) : 8, :], rows)
         words.append(load_words(1, late, offset=CHUNK))
         second = load_held_dw(1, 0, M)
         words.append(load_words(2, late, offset=2 * CHUNK))

from contextlib import ExitStack

import concourse.mybir as mybir

K, M, T, S = 2048, 512, 2048, 512
FLOPS = 2 * 2 * K * M * S

F32 = mybir.dt.float32
BF16 = mybir.dt.bfloat16
I32 = mybir.dt.int32
U32 = mybir.dt.uint32
U16 = mybir.dt.uint16
U8 = mybir.dt.uint8
FP8X4 = mybir.dt.float8_e4m3fn_x4
FP4X4 = mybir.dt.float4_e2m1fn_x4
GELU = mybir.ActivationFunctionType.Gelu_apprx_tanh

P = 128
PASSES = K // 512
TILES = M // P
LAST = PASSES - 1
CHUNK = 4 * T
HALF = S // 2
ROW0 = 32


def tile_list_tabd_gelu_kernel(tc, tab, w4_words, w4_scales, dw, b, offs, out):
    nc = tc.nc
    with ExitStack() as ctx:
        keep = ctx.enter_context(tc.tile_pool(name="keep", bufs=1))
        late = ctx.enter_context(tc.tile_pool(name="late", bufs=1))
        psum = ctx.enter_context(tc.psum_pool(name="psum", bufs=1))

        offsets = keep.tile([P, S // 16], U16, name="offsets")
        held = late.tile([P, 7 * CHUNK], U8, name="held", align_bytes=256, offset=0)
        window = held[:, 0:T]
        picked = keep.tile([P, S], U8, name="picked", align_bytes=256)
        planes = keep.tile([P, PASSES, S], U8, name="planes", align_bytes=256)
        w4_planes = keep.tile([P, PASSES, M], U8, name="w4_planes", align_bytes=256)
        bias_rows = keep.tile([P, 32], F32, name="bias_rows", align_bytes=256)
        nc.vector.memset(w4_planes[:].bitcast(I32), 0)
        nc.vector.memset(bias_rows[:], 0.0)
        nc.vector.memset(window[0:ROW0, :].bitcast(I32), 0)
        nc.vector.memset(window[ROW0 + 64 : P, :].bitcast(I32), 0)
        nc.vector.memset(planes[:].bitcast(I32), 0)

        warm = keep.tile([P, 1], F32, name="warm")
        nc.vector.memset(warm[:], 0.0)
        warm_out = keep.tile([P, 1], F32, name="warm_out")
        nc.scalar.activation(warm_out[:], warm[:], GELU)

        def place(a, c0):
            return {1: 0, 2: 4, LAST: 5}[a] * CHUNK + 16 * c0

        def load_dw(a, c0, c1, pool, **where):
            piece = pool.tile([P, 4, c1 - c0], F32, name=f"dw{a}_{c0}", align_bytes=256, **where)
            nc.sync.dma_start(piece[:], dw[512 * a : 512 * (a + 1), c0:c1].rearrange("(p j) n -> p j n", j=4))
            return piece

        def load_held_dw(a, c0, c1):
            return load_dw(a, c0, c1, late, offset=place(a, c0))

        def load_words(a, pool, **where):
            tile = pool.tile([P, T], I32, name=f"words{a}", align_bytes=256, **where)
            nc.sync.dma_start(tile[:], tab[a, 0 : 512 * T].rearrange("(p n) -> p n", p=P).bitcast(I32))
            return tile

        nc.sync.dma_start(
            window[ROW0 : ROW0 + 64, :].bitcast(I32),
            tab[:, 512 * T : 528 * T].rearrange("a (g t) -> g a t", t=T).bitcast(I32),
        )
        nc.sync.dma_start(offsets[:], offs)
        words = [load_words(0, keep)]
        for r in range(4):
            nc.sync.dma_start(
                w4_planes[r:P:32, :, :].bitcast(I32),
                w4_scales[:, r:16:4, :].rearrange("a q n -> q a n").bitcast(I32),
            )
        w4 = {}

        def load_w4(a0, a1, m0, m1, pool, **where):
            tile = pool.tile([P, a1 - a0, 2 * P * (m1 - m0)], U8, name=f"w4_{a0}_{m0}", align_bytes=256, **where)
            rows = w4_words[a0:a1, :, 2 * P * m0 : 2 * P * m1].rearrange("a p n -> p a n")
            nc.sync.dma_start(tile[:].bitcast(I32), rows.bitcast(I32))
            for a in range(a0, a1):
                for m in range(m0, m1):
                    w4[a, m] = tile[:, a - a0, 2 * P * (m - m0) : 2 * P * (m - m0 + 1)]

        load_w4(0, 2, 0, TILES, keep)
        load_w4(2, PASSES, 0, TILES, keep)
        whole = load_dw(0, 0, M, keep)

        nc.vector.tensor_copy(picked[:], window.indirect(offsets[:]))
        for q in (0, 2, 1, 3):
            nc.sync.dma_start(
                planes[32 * q : 32 * q + 4, :, :].bitcast(I32),
                picked[ROW0 + 16 * q : ROW0 + 16 * (q + 1), :].bitcast(I32),
            )

        for h in range(2):
            rows = b.rearrange("(m q i) -> q m i", q=4, i=32)[2 * h : 2 * h + 2]
            nc.sync.dma_start(bias_rows[64 * h : 64 * (h + 1) : 8, :], rows)
        words.append(load_words(1, late, offset=CHUNK))
        second = load_held_dw(1, 0, M)
        words.append(load_words(2, late, offset=2 * CHUNK))
        words.append(load_words(LAST, late, offset=LAST * CHUNK))
        left = {a: load_held_dw(a, 0, 2 * P) for a in (2, LAST)}
        right = {(a, m): load_held_dw(a, P * m, P * (m + 1)) for a, m in ((2, 2), (LAST, 2), (2, 3))}
        ends = [load_held_dw(LAST, c, c + P // 2) for c in (3 * P, 3 * P + P // 2)]

        banks = {m: [(psum.tile([P, S], F32, name=f"acc{m}"), 0, S)] for m in range(TILES - 1)}
        banks[TILES - 1] = [
            (psum.tile([P, HALF], F32, name=f"acc_last{h}"), HALF * h, HALF * (h + 1)) for h in range(2)
        ]
        gathered = [keep.tile([P, S], U32, name=f"gathered{a}", align_bytes=256) for a in range(PASSES)]

        def one_pass(a, m, lhsT, lhsT_scale, start, stop, which=slice(None)):
            for acc, c0, c1 in banks[m][which]:
                nc.tensor.matmul_mx(
                    out=acc[:],
                    lhsT=lhsT,
                    lhsT_scale=lhsT_scale,
                    rhs=gathered[a][:, c0:c1].bitcast(FP8X4),
                    rhs_scale=planes[:, a, c0:c1],
                    start=start,
                    stop=stop,
                )

        def w4_pass(a, m, stop=False, which=slice(None)):
            one_pass(a, m, w4[a, m].bitcast(FP4X4), w4_planes[:, a, P * m : P * (m + 1)], a == 0, stop, which)

        def w4_passes(a):
            nc.vector.tensor_copy(gathered[a][:], words[a][:].bitcast(U32).indirect(offsets[:]))
            for m in range(TILES):
                w4_pass(a, m)

        def weave(src, a, m0, copies):
            width = src.shape[2]
            share = width // len(copies)
            dst = keep.tile([P, width, 4], BF16, name=f"woven{a}_{m0}", align_bytes=256)
            for n, copy in enumerate(copies):
                cols = slice(share * n, share * (n + 1))
                copy(
                    dst[:, cols, :].rearrange("p (c i) j -> p c j i", i=2),
                    src[:, :, cols].rearrange("p j (c i) -> p c j i", i=2),
                )
            return dst

        def quantise(woven, a, m0, pool=keep, **where):
            width = woven.shape[1]
            codes = pool.tile([P, width], U32, name=f"codes{a}_{m0}", align_bytes=256, **where)
            scales = keep.tile([P, width], U8, name=f"scales{a}_{m0}", align_bytes=256)
            nc.vector.quantize_mx(
                out=codes[:].bitcast(FP8X4), scales=scales[:], in_=woven[:].rearrange("p n j -> p (n j)")
            )
            return codes, scales

        def dw_passes(woven, a, m0, stop):
            codes, scales = quantise(woven, a, m0)
            for i in range(woven.shape[1] // P):
                cols = slice(P * i, P * (i + 1))
                one_pass(a, m0 + i, codes[:, cols].bitcast(FP8X4), scales[:, cols], False, stop)

        def change(src, a, m0, copies):
            dw_passes(weave(src, a, m0, copies), a, m0, a == LAST)

        def finish(m, pool=keep, **where):
            res = pool.tile([P, S], F32, name=f"res{m}", align_bytes=256, **where)
            for acc, c0, c1 in banks[m]:
                nc.scalar.activation(res[:, c0:c1], acc[:], GELU, bias=bias[:, 8 * m : 8 * m + 1])
                nc.sync.dma_start(out[P * m : P * (m + 1), c0:c1], res[:, c0:c1])

        vector, scalar = nc.vector.tensor_copy, nc.scalar.copy
        for a, tile in ((0, whole), (1, second)):
            w4_passes(a)
            change(tile[:, :, 2 * P : M], a, 2, (vector,))
            change(tile[:, :, 0 : 2 * P], a, 0, (scalar,))
        bias = second[:, 0, 0:32]
        nc.vector.transpose(bias, bias_rows[:])
        for a in (2, LAST):
            w4_passes(a)
        for a in (2, LAST):
            change(left[a][:, :, P : 2 * P], a, 1, (vector,))
            change(left[a][:, :, 0:P], a, 0, (scalar,))
        change(right[2, 2][:], 2, 2, (scalar,))
        finish(1)
        finish(0)
        change(right[LAST, 2][:], LAST, 2, (vector,))
        finish(2)
        ahead = weave(right[2, 3][:], 2, 3, (vector,))
        final = keep.tile([P, P, 4], BF16, name="woven_final", align_bytes=256)
        for n, piece in enumerate(ends):
            vector(
                final[:, P // 2 * n : P // 2 * (n + 1), :].rearrange("p (c i) j -> p c j i", i=2),
                piece[:].rearrange("p j (c i) -> p c j i", i=2),
            )
        ahead_codes, ahead_scales = quantise(ahead, 2, 3, late, offset=place(LAST, 3 * P + P // 2))
        final_codes, final_scales = quantise(final, LAST, 3)
        for h in range(2):
            bank = slice(h, h + 1)
            one_pass(2, 3, ahead_codes[:].bitcast(FP8X4), ahead_scales[:], False, False, bank)
            one_pass(LAST, 3, final_codes[:].bitcast(FP8X4), final_scales[:], False, True, bank)
        finish(3)
